import numpy as np, ml_dtypes
CORES = [48,51,52,55]
N = 4
BF = ml_dtypes.bfloat16
def gentries(a):
    return np.ascontiguousarray(a.reshape(8, 16, -1).transpose(0, 2, 1)).reshape(8, -1)
def gtable(e):
    e = np.asarray(e); return np.ascontiguousarray(e.reshape(8, -1, 16).transpose(0, 2, 1)).reshape(128, -1).astype(np.int32)
S, n, M, CAP, DM = 3, 2048, 16, 320, 63
def lists(prev, ship, heads):
    a = [np.stack([gentries(x) for x in v]).astype(np.int64) for v in (prev, ship, heads)]
    return a[0].reshape(N, 8, S - 1, n), a[1].reshape(N, 8, S - 1, N, CAP), a[2].reshape(N, 8, S, M)
def before(pv, sh):
    r = np.arange(N).reshape(-1, 1, 1, 1); g = np.arange(8).reshape(1, -1, 1, 1); t = np.arange(S - 1).reshape(1, 1, -1, 1)
    x = np.maximum(pv - n, 0); q = x // CAP; e = sh[q, g, t, r, x % CAP]
    return np.where(pv < n, r * n + pv, np.where(e < 0, -1, q * n + e))
def counts(rng, w, swaps):
    A = np.zeros((N, N), np.int64); i = np.arange(N)
    for k in range(1, N): A[i, (i + k) % N] = w[k - 1]
    A[i, i] = n - np.add.reduce(A, axis=1)
    lim = np.where(np.eye(N, dtype=bool), n, CAP)
    for k in range(swaps):
        a, b = rng.permutation(N)[:2]; c, e = rng.permutation(N)[:2]
        m = int(min(A[a, e], A[b, c], lim[a, c] - A[a, c], lim[b, e] - A[b, e])); x = int(rng.integers(0, m // 3 + 1))
        A[a, c] += x; A[b, e] += x; A[a, e] -= x; A[b, c] -= x
    return A
def mixed(rng):
    return [[counts(rng, rng.integers(CAP // 4, 3 * CAP // 4, N - 1), 3 * N) for g in range(8)] for t in range(S - 1)]
def evens(rng):
    h = np.arange(M) * (n // M) + rng.integers(-(n // M // 3), n // M // 3 + 1, (N, 8, S, M)); h[..., 0] = 0
    return h
def uneven(rng):
    m = np.arange(M); b = rng.integers(0, M, (N, 8, S, 1))
    return np.where(m <= b, m, n - M + m)
def shop(rng, hd, ways, noise, turn=False):
    pv = np.zeros((N, 8, S - 1, n), np.int64); sh = np.full((N, 8, S - 1, N, CAP), -1, np.int64); ph = np.zeros((N, 8, S, n), np.int64); i = np.arange(n)
    for r in range(N):
        for g in range(8):
            for t in range(S):
                h = hd[r, g, t]; m = np.searchsorted(h, i, side="right") - 1; size = np.append(h, n)[1:] - h
                ph[r, g, t] = (2 * (i - h[m]) + 1) * 32768 // size[m]
    for t in range(S - 1):
        for g in range(8):
            A = ways[t][g]; num = [[] for r in range(N)]; key = [[] for r in range(N)]
            for q in range(N):
                o = rng.permutation(n); e = np.add.accumulate(A[q])
                for r in range(N):
                    u = o[e[r] - A[q, r]:e[r]]
                    if r == q: num[r].append(u)
                    else:
                        sh[q, g, t, r, :len(u)] = u; num[r].append(n + CAP * q + np.arange(len(u)))
                    key[r].append(ph[q, g, t, u])
            for r in range(N):
                a = np.concatenate(num[r]); k = np.concatenate(key[r]) + rng.integers(-noise, noise + 1, n)
                if turn: k = 65536 - k
                place = np.argsort(ph[r, g, t + 1] * n + rng.permutation(n))
                pv[r, g, t, place] = a[np.argsort(k)]
    return {"prev": np.stack([gtable(x.reshape(8, -1)) for x in pv]), "ship": np.stack([gtable(x.reshape(8, -1)) for x in sh]), "heads": np.stack([gtable(x.reshape(8, -1)) for x in hd])}
def times_of(rng):
    top = rng.integers(15, DM + 1, (N, 128, 1))
    return np.floor(rng.random((N, 128, S * n)) * (top + 1)).astype(BF)
def setup_inputs(rng):
    return {"dur": times_of(rng), **shop(rng, evens(rng), mixed(rng), 1500)}
def setup_inputs_full(rng):
    ways = [[counts(rng, [[CAP] * (N - 1), [0] * (N - 1), [CAP] + [0] * (N - 2), [1] * (N - 1)][(g + t) % 4], 0) for g in range(8)] for t in range(S - 1)]
    return {"dur": times_of(rng), **shop(rng, evens(rng), ways, 1500)}
def setup_inputs_machines(rng):
    hd = uneven(rng)
    return {"dur": rng.integers(DM - 15, DM + 1, (N, 128, S * n)).astype(np.float32).astype(BF), **shop(rng, hd, mixed(rng), 1 << 20)}
def setup_inputs_turned(rng):
    ways = mixed(rng)
    for t in range(S - 1):
        for g in range(0, 8, 2): ways[t][g] = counts(rng, [0] * (N - 1), 0)
    return {"dur": np.full((N, 128, S * n), DM, np.float32).astype(BF), **shop(rng, uneven(rng), ways, 0, turn=True)}
def setup_inputs_ties(rng):
    c = rng.integers(1, DM + 1, (N, 128, 1)); z = rng.integers(0, 4, (N, 128, S * n)) > 0; z[:, ::2] = True
    c[:, ::2] = 8
    return {"dur": np.where(z, c, 0).astype(np.float32).astype(BF), **shop(rng, evens(rng), mixed(rng), 1500)}
def setup_inputs_spread(rng):
    e = rng.integers(0, 7, (N, 1, S * n))
    return {"dur": np.floor(rng.random((N, 128, S * n)) * np.exp2(e)).astype(BF), **shop(rng, evens(rng), mixed(rng), 6000)}
def check_inputs(d):
    bad = []; v = d["dur"].astype(np.float32)
    if not (np.isfinite(v).all() and (v >= 0).all() and (v <= DM).all() and (v == np.floor(v)).all()): bad.append("durations")
    pv, sh, hd = lists(d["prev"], d["ship"], d["heads"])
    if (hd[..., 0] != 0).any() or (hd[..., 1:] <= hd[..., :-1]).any() or (hd[..., -1] >= n).any(): bad.append("heads")
    own = np.arange(N)
    if (sh < -1).any() or (sh >= n).any() or ((sh[..., 1:] >= 0) & (sh[..., :-1] < 0)).any() or (sh[own, :, :, own] != -1).any(): bad.append("ship")
    if (pv < 0).any() or (pv >= n + N * CAP).any(): bad.append("prev")
    if bad: return bad
    b = np.sort(before(pv, sh).transpose(1, 2, 0, 3).reshape(8, S - 1, N * n), axis=-1)
    if (b != np.arange(N * n)).any() or np.count_nonzero(sh >= 0) != np.count_nonzero(pv >= n): bad.append("jobs")
    return bad
def reference(dur, prev, ship, heads):
    pv, sh, hd = lists(prev, ship, heads); g = np.arange(8)
    b = before(pv, sh).transpose(2, 3, 0, 1)
    d = np.ascontiguousarray(dur.astype(np.float32).astype(np.int64).reshape(N, 8, 16, S, n).transpose(3, 4, 0, 1, 2))
    st = np.zeros((N, 8, S, n), bool); np.put_along_axis(st, hd, True, axis=-1)
    st = np.ascontiguousarray(st.transpose(2, 3, 0, 1))[..., None]
    C = np.zeros((S, n, N, 8, 16), np.int64)
    for t in range(S):
        R = np.zeros((n, N, 8, 16), np.int64) if t == 0 else C[t - 1].transpose(1, 0, 2, 3).reshape(N * n, 8, 16)[b[t - 1], g]
        m = np.zeros((N, 8, 16), np.int64)
        for i in range(n):
            m = np.maximum(np.where(st[t, i], 0, m), R[i]) + d[t, i]; C[t, i] = m
    D = np.max(C[S - 1], axis=(0, 1))
    sl = np.zeros((S - 1, n, N, 8, 16), np.int64); B = np.zeros((n, N, 8, 16), np.int64)
    for t in range(S - 1, -1, -1):
        if t == S - 1: Q = np.broadcast_to(D, (n, N, 8, 16))
        else:
            w = np.zeros((N * n, 8, 16), np.int64); w[b[t], g] = B; Q = w.reshape(N, n, 8, 16).transpose(1, 0, 2, 3)
        B = np.zeros((n, N, 8, 16), np.int64); m = np.broadcast_to(D, (N, 8, 16))
        for i in range(n - 1, -1, -1):
            F = np.minimum(m, Q[i])
            if t < S - 1: sl[t, i] = F - C[t, i]
            B[i] = F - d[t, i]; m = np.where(st[t, i], D, B[i])
    y = sl.transpose(2, 3, 4, 0, 1).reshape(N, 128, (S - 1) * n)
    return {"y": y.astype(np.float32)}

@@ -1,0 +1,323 @@
+from concourse.bass import DstId, RemoteDMATransfer
+from concourse.mybir import AluOpType as Op, AxisListType as Ax, ActivationFunctionType as Fn
+
+N, n, CAP = 4, 2048, 320
+BIG = float(1 << 20)
+LC = CAP // 16
+SL = N * LC
+SP = 1392
+JB = 64
+RD = 256
+NCH = 4
+CH = n // NCH
+JC = [0, 384, 2048]
+C0 = [0, 1024, 2048]
+C2 = [0, 1536, 2048]
+ORDER = ["d2", "d0", "s1", "iw", "d0", "d2", "s2", "d1"]
+DPOS = 2
+TAIL = "u0 d0 a0 u1 a1 u2 b3 a2 b2 u3 b1 A3 b0"
+
+SCRATCH = {
+    "d0": ("sbuf", [128, n], "bfloat16"), "d2": ("sbuf", [128, n], "bfloat16"), "d1": ("sbuf", [128, n + 16], "bfloat16"),
+    "m0": ("sbuf", [128, n + 16], "bfloat16"), "m2": ("sbuf", [128, n + 16], "bfloat16"), "z0": ("sbuf", [128, n + 16], "bfloat16"),
+    "kz": ("sbuf", [128, 16], "bfloat16"), "kn": ("sbuf", [128, 16], "bfloat16"), "kp": ("sbuf", [128, 16], "bfloat16"),
+    "hd": ("sbuf", [128, 3], "int32"), "hu": ("sbuf", [128, 6], "uint16"),
+    "la": ("sbuf", [128, SL + 256], "int32"), "lb": ("sbuf", [128, SL], "int32"),
+    "tr": ("sbuf", [128, SL], "int32"), "tq": ("sbuf", [128, SL], "int32"),
+    "pa": ("sbuf", [128, 128], "int32"), "pb": ("sbuf", [128, SL], "int32"), "pc": ("sbuf", [128, SL], "int32"),
+    "oa": ("sbuf", [128, SL + 256], "uint16"), "ob": ("sbuf", [128, 128], "uint16"), "oc": ("sbuf", [128, SL], "uint16"),
+    "od": ("sbuf", [128, SL], "uint16"), "oi": ("sbuf", [128, 208], "uint16"),
+    "cw": ("sbuf", [128, n + N * CAP], "float32"), "sb1": ("sbuf", [128, (N - 1) * CAP], "float32"),
+    "g2": ("sbuf", [128, n], "float32"), "w2": ("sbuf", [128, SP + n + N * CAP], "float32"), "r2": ("sbuf", [128, (N - 1) * CAP], "float32"),
+    "rr": ("sbuf", [128, n], "float32"), "ss": ("sbuf", [128, n], "float32"), "gp": ("psum", [128, n], "float32"),
+    "vw": ("sbuf", [128, n + N * CAP], "float32"), "sb3": ("sbuf", [128, (N - 1) * CAP], "float32"),
+    "iw": ("sbuf", [128, 4096 + SP], "float32"), "jj": ("sbuf", [128, n + (N - 1) * CAP], "float32"),
+    "fz": ("sbuf", [128, CAP], "float32"), "it": ("sbuf", [128, 256], "float32"),
+    "uu": ("sbuf", [128, n], "float32"), "a0": ("sbuf", [128, n], "float32"), "y0": ("sbuf", [128, n], "float32"),
+    "fx": ("sbuf", [128, 16], "float32"), "tm": ("sbuf", [128, 16], "float32"),
+    "dq": ("sbuf", [128, 4 * N], "float32"), "dc": ("sbuf", [128, 4], "float32"),
+}
+SEMAPHORES = ["a1", "a20", "a21", "a22", "a3", "a4", "sent"] + ["e%d" % k for k in range(135)]
+
+
+def rank_program(g, core, T, topo):
+    r = T.rank_of(core)
+    if r is None:
+        return
+    cores = list(T.cores)
+    turn = [(r + 1 + k) % N for k in range(N - 1)]
+    frm = [(r - 1 - k) % N for k in range(N - 1)]
+    V, A, S = g.vector, g.scalar, g.sync
+    nxt = [0]
+    seen = {}
+    made = []
+    sent = [0]
+
+    def ev(ins, k=1):
+        name = "e%d" % nxt[0]
+        nxt[0] += 1
+        ins.then_inc(T.sem[name], k)
+        made.append((name, k))
+        return (name, k)
+
+    def wait(q, qn, *evs):
+        for e in evs:
+            if (qn, e) not in seen:
+                seen[(qn, e)] = True
+                seen[e] = True
+                q.wait_ge(T.sem[e[0]], e[1])
+
+    def vw(*e): wait(V, "v", *e)
+    def aw(*e): wait(A, "a", *e)
+    def sw(*e): wait(S, "s", *e)
+    def gw(*e): wait(g, "g", *e)
+
+    def engines(p, q):
+        return len(topo.engines(cores[p], cores[q]))
+
+    def send(q, dst, src, sem):
+        rid, pid, _ = topo.addr(cores[q])
+        g.remote_dma(dst, src, T.sem[sem], T.sem.sent, pid, rid, topo.mask(core, cores[q]))
+        sent[0] += engines(r, q)
+
+    def slot(t, k, base=0):
+        return t[:, base + k * CAP:base + (k + 1) * CAP]
+
+    def cols(t, q, base=0):
+        return t[:, base + q * LC:base + (q + 1) * LC]
+
+    l_hd = ev(A.dma_start(T.hd[:], T.heads[:]), 16)
+    l_pv = ev(A.dma_start(T.la[:, SL:SL + 256], T.prev[:]), 16)
+    f_fz = ev(V.memset(T.fz[:], float(JB)))
+    f_m2 = ev(V.memset(T.m2[:], 1.0))
+    l_d0, l_d2, ld = [], [], {}
+    for w in ORDER:
+        if w == "d0":
+            k = len(l_d0)
+            l_d0.append(ev(S.dma_start(T.d0[:, C0[k]:C0[k + 1]], T.dur[:, C0[k]:C0[k + 1]]), 16))
+        elif w == "d2":
+            k = len(C2) - 2 - len(l_d2)
+            l_d2.append(ev(S.dma_start(T.d2[:, C2[k]:C2[k + 1]], T.dur[:, 2 * n + C2[k]:2 * n + C2[k + 1]]), 16))
+        elif w == "iw":
+            sw(f_fz)
+            ld[w] = ev(S.dma_start(T.iw[::16, 0:4096], T.fz[:, 0:256]), 16)
+        elif w == "s1":
+            ld[w] = ev(S.dma_start(T.la[:, 0:SL], T.ship[:, 0:SL]), 16)
+        elif w == "s2":
+            ld[w] = ev(S.dma_start(T.lb[:], T.ship[:, SL:2 * SL]), 16)
+        else:
+            ld[w] = ev(S.dma_start(T.d1[:, 16:16 + n], T.dur[:, n:2 * n]), 16)
+
+    def const(ap, k, v):
+        return ev(g.iota(ap, [[0, k]], v, 0, allow_small_or_imprecise_dtypes=True))
+
+    def count(lo, hi, base):
+        return ev(g.iota(T.jj[:, lo:hi], [[1, hi - lo]], base, 0, allow_small_or_imprecise_dtypes=True))
+    f_kz = const(T.kz[:], 16, 0)
+    f_j = [count(JC[k], JC[k + 1], JB + JC[k]) for k in range(len(JC) - 1)]
+    f_tr = ev(g.iota(T.tr[:], [[16, SL]], 4096, 1))
+    f_tq = ev(g.iota(T.tq[:], [[16, SL]], 4096 - SP, 1))
+    f_kn = const(T.kn[:], 16, -int(BIG))
+
+    aw(f_fz)
+    f_w2 = [ev(A.activation(slot(T.w2, q, SP + n), T.fz[:], Fn.Identity)) for q in turn]
+    f_cw = ev(A.activation(slot(T.cw, r, n), T.fz[:], Fn.Identity))
+
+    g2, sc2 = [], []
+
+    def span2(k):
+        return C2[-2 - k], C2[-1 - k]
+
+    def scan2(k):
+        lo, hi = span2(k)
+        rev = slice(hi - 1, lo - 1 if lo else None, -1)
+        vw(l_d2[k], x_m2, *g2[-1:])
+        g2.append(ev(V.tensor_tensor_scan(T.g2[:, rev], T.m2[:, hi:lo:-1], T.d2[:, rev], T.g2[:, hi:hi + 1] if k else 0.0, Op.mult, Op.add)))
+
+    def scatter2(k):
+        lo, hi = span2(k)
+        vw(x_op, g2[k], *f_w2, *sc2[-1:])
+        sc2.append(ev(V.tensor_copy(T.w2[:, SP:SP + n + N * CAP].indirect(T.oa[:, SL + 128 + lo // 16:SL + 128 + hi // 16]), T.g2[:, lo:hi])))
+
+    vw(l_hd)
+    x_hu = ev(V.tensor_copy(T.hu[:, 0:6:2], T.hd[:]))
+    vw(x_hu, f_m2, f_kz)
+    x_m2 = ev(V.tensor_copy(T.m2[:, 0:n].indirect(T.hu[:, 4:5]), T.kz[:]))
+    aw(x_m2)
+    f_m0 = ev(A.activation(T.m0[:], T.m2[:], Fn.Identity, bias=1.0, scale=0.0))
+    scan2(0)
+    vw(l_pv)
+    x = ev(V.tensor_scalar(T.pa[:], T.la[:, SL:SL + 128], 4097, None, Op.mult))
+    x_op = ev(V.tensor_copy(T.oa[:, SL:SL + 256], T.la[:, SL:SL + 256]))
+    vw(x)
+    x = ev(V.tensor_scalar(T.pa[:], T.pa[:], 4, 0xFFF, Op.arith_shift_right, Op.bitwise_and))
+    vw(x)
+    x_ob = ev(V.tensor_copy(T.ob[:], T.pa[:]))
+    scatter2(0)
+    vw(f_m0)
+    x_m0 = ev(V.tensor_copy(T.m0[:, 0:n].indirect(T.hu[:, 0:1]), T.kz[:]))
+    vw(ld["s1"])
+    x_oa = ev(V.tensor_copy(T.oa[:, 0:SL], T.la[:, 0:SL]))
+    c0 = []
+    vw(x_m0)
+    for k in range(len(C0) - 1):
+        lo, hi = C0[k], C0[k + 1]
+        vw(l_d0[k], *c0[-1:])
+        c0.append(ev(V.tensor_tensor_scan(T.cw[:, lo:hi], T.m0[:, lo:hi], T.d0[:, lo:hi], T.cw[:, lo - 1:lo] if k else 0.0, Op.mult, Op.add)))
+    for k in range(1, len(C2) - 1):
+        scan2(k)
+        scatter2(k)
+    sc2 = sc2[-1]
+
+    last = [ld["iw"]]
+
+    def index_scatter(off, src, *ready):
+        aw(last[0], *ready)
+        last[0] = ev(A.activation(T.iw[:].indirect(off), src, Fn.Silu))
+
+    def prev_piece(k):
+        index_scatter(T.ob[:, JC[k] // 16:JC[k + 1] // 16], T.jj[:, JC[k]:JC[k + 1]], x_ob, f_j[k])
+
+    prev_piece(0)
+    aw(x_oa, *c0)
+    for k, q in enumerate(turn):
+        gw(ev(A.activation(slot(T.sb1, k), T.cw[:, 0:n].indirect(cols(T.oa, q)), Fn.Identity)))
+        send(q, slot(T.cw, r, n), slot(T.sb1, k), "a1")
+    a1 = ("a1", sum(engines(q, r) for q in frm))
+    f_js = count(n, n + (N - 1) * CAP, JB + n)
+    for k in range(1, len(JC) - 1):
+        prev_piece(k)
+
+    gw(sc2)
+    for k, q in enumerate(turn):
+        send(q, slot(T.r2, k), slot(T.w2, q, SP + n), "a2%d" % k)
+    f_kp = const(T.kp[:], 16, int(BIG))
+    f_d1 = const(T.d1[:, 0:16], 16, 0)
+    f_z0 = const(T.z0[:], n + 16, 0)
+
+    x1 = ev(V.tensor_scalar(T.pb[:], T.la[:, 0:SL], 4097, None, Op.mult))
+    vw(ld["s2"])
+    x2 = ev(V.tensor_scalar(T.pc[:], T.lb[:], 4096, None, Op.mult))
+    vw(x1)
+    x1 = ev(V.tensor_scalar(T.pb[:], T.pb[:], 4, 0x100FFF, Op.arith_shift_right, Op.bitwise_and))
+    vw(x2, f_tq)
+    x2 = ev(V.tensor_tensor(T.pc[:], T.pc[:], T.tq[:], Op.add))
+    vw(x1, f_tr)
+    x1 = ev(V.tensor_tensor(T.pb[:], T.pb[:], T.tr[:], Op.min))
+    vw(ld["d1"])
+    fx = ev(V.tensor_scalar(T.fx[:], T.d1[:, 16:16 + n].indirect(T.hu[:, 2:3]), BIG, None, Op.add))
+    vw(x1)
+    x_od = ev(V.tensor_copy(T.od[:], T.pb[:]))
+    vw(x2)
+    x2 = ev(V.tensor_tensor(T.pc[:], T.pc[:], T.lb[:], Op.min))
+    vw(fx, f_kn)
+    x_d1 = ev(V.tensor_copy(T.d1[:, 16:16 + n].indirect(T.hu[:, 2:3]), T.kn[:]))
+    vw(x2)
+    x_oc = ev(V.tensor_scalar(T.oc[:], T.pc[:], SP, None, Op.add))
+    RA = n - RD
+    rs = []
+    if RD:
+        vw(a1, f_cw)
+        rs.append(ev(V.tensor_copy(T.rr[:, RA:n], T.cw[:].indirect(T.oa[:, SL + RA // 16:SL + 128]))))
+
+    for k, q in enumerate(frm):
+        index_scatter(cols(T.od, q), slot(T.jj, k, n), x_od, f_js)
+    aw(a1, f_cw, x_op)
+    rs.append(ev(A.activation(T.rr[:, 0:RA], T.cw[:].indirect(T.oa[:, SL:SL + RA // 16]), Fn.Identity)))
+    sw(last[0])
+    l_it = ev(S.dma_start(T.it[:], T.iw[::16, 0:4096]), 16)
+
+    sh2 = sc2
+    for k, q in enumerate(frm):
+        vw(("a2%d" % k, engines(q, r)), sh2, x_oc)
+        sh2 = ev(V.tensor_copy(T.w2[:, 0:SP + n].indirect(cols(T.oc, q)), slot(T.r2, k)))
+    vw(sh2, x_d1)
+    g1 = ev(V.tensor_tensor_scan(T.gp[:, ::-1], T.w2[:, SP + n - 1:SP - 1:-1], T.d1[:, n + 15:15:-1], 0.0, Op.max, Op.add))
+    vw(*rs)
+    x = ev(V.tensor_tensor(T.tm[:], T.rr[:].indirect(T.hu[:, 2:3]), T.fx[:], Op.add))
+    vw(l_it)
+    x_oi = ev(V.tensor_scalar(T.oi[:], T.it[:, 0:208], 0.25 - JB, None, Op.add))
+    vw(x)
+    rfix = ev(V.tensor_copy(T.rr[:].indirect(T.hu[:, 2:3]), T.tm[:]))
+    vw(g1, rfix)
+    vv = ev(V.tensor_tensor(T.vw[:, 0:n], T.gp[:], T.rr[:], Op.add))
+    mine = T.dq[:, 4 * r:4 * r + 1]
+    vw(vv)
+    red = ev(V.tensor_reduce(mine, T.vw[:, 0:n], Ax.X, Op.max))
+
+    aw(vv, x_oi)
+    ids = [DstId(rid=topo.addr(cores[q])[0], pnc=topo.addr(cores[q])[1]) for q in turn]
+
+    def send_max():
+        gw(red)
+        g.remote_dma_fused([RemoteDMATransfer(dst_ids=ids, dma_engine_mask=topo.mask(core, cores[turn[0]]), remote_sem=T.sem.a4,
+                                              srcs=[mine], dsts=[mine for p in turn])], local_sem=T.sem.sent)
+        sent[0] += engines(r, turn[0])
+    for k, q in enumerate(turn):
+        e = ev(A.activation(slot(T.sb3, k), T.vw[:, 0:n].indirect(cols(T.oi, q, 128)), Fn.Identity))
+        if k == DPOS:
+            send_max()
+        gw(e)
+        send(q, slot(T.vw, k, n), slot(T.sb3, k), "a3")
+    if DPOS >= N - 1:
+        send_max()
+    a3 = ("a3", sum(engines(q, r) for q in frm))
+    a4 = ("a4", sum(engines(q, (q + 1) % N) for q in frm))
+
+    vw(f_d1)
+    ss = ev(V.tensor_tensor_scan(T.ss[:], T.d1[:, 15:15 + n], T.rr[:], 0.0, Op.add, Op.max))
+    vw(f_z0, f_kp)
+    x_z0 = ev(V.tensor_copy(T.z0[:, 0:n].indirect(T.hu[:, 0:1]), T.kp[:]))
+    us, ga, sc, dd = {}, {}, {}, []
+    D = T.dc[:, 0:1]
+
+    def u_piece(k):
+        vw(ss)
+        us[k] = ev(V.tensor_tensor(T.uu[:, k * CH:(k + 1) * CH], T.gp[:, k * CH:(k + 1) * CH], T.ss[:, k * CH:(k + 1) * CH], Op.add))
+
+    def d_piece():
+        vw(a4, red)
+        dd.append(ev(V.tensor_reduce(D, T.dq[:, ::4], Ax.X, Op.max)))
+        aw(a3, *dd)
+        for k in range(NCH - 1, -1, -1):
+            ga[k] = ev(A.activation(T.a0[:, k * CH:(k + 1) * CH],
+                                    T.vw[:, 0:n + (N - 1) * CAP].indirect(T.oi[:, k * CH // 16:(k + 1) * CH // 16]),
+                                    Fn.Identity, bias=D, scale=-1.0))
+
+    def store(e, col, src):
+        sw(e)
+        ev(S.dma_start(T.y[:, col:col + CH], src), 16)
+
+    def s1_piece(k, on_v):
+        ap = T.uu[:, k * CH:(k + 1) * CH]
+        if on_v:
+            vw(us[k], *dd)
+            e = ev(V.tensor_scalar(ap, ap, -1.0, D, Op.mult, Op.add))
+        else:
+            aw(us[k])
+            e = ev(A.activation(ap, ap, Fn.Identity, bias=D, scale=-1.0))
+        store(e, n + k * CH, ap)
+
+    def s0_piece(k):
+        lo, hi = k * CH, (k + 1) * CH
+        rev = slice(hi - 1, lo - 1 if lo else None, -1)
+        vw(ga[k], x_z0)
+        if k < NCH - 1:
+            vw(sc[k + 1])
+        sc[k] = ev(V.tensor_tensor_scan(T.y0[:, rev], T.z0[:, hi:lo:-1], T.a0[:, rev],
+                                        BIG if k == NCH - 1 else T.y0[:, hi:hi + 1], Op.max, Op.min))
+        store(sc[k], lo, T.y0[:, lo:hi])
+
+    for w in TAIL.split():
+        k = int(w[1:])
+        if w[0] == "u":
+            u_piece(k)
+        elif w[0] == "d":
+            d_piece()
+        elif w[0] == "b":
+            s0_piece(k)
+        else:
+            s1_piece(k, w[0] == "a")
+
+    gw(("sent", sent[0]))
+    sw(*[e for e in made if e not in seen])

@@ -1,43 +1,48 @@
-from concourse.bass import DstId, RemoteDMATransfer
 from concourse.mybir import AluOpType as Op, AxisListType as Ax, ActivationFunctionType as Fn
 
 N, n, CAP = 4, 2048, 320
 BIG = float(1 << 20)
+RND = float(3 << 22)
 LC = CAP // 16
 SL = N * LC
 SP = 1392
 JB = 64
-RD = 256
-NCH = 4
-CH = n // NCH
-JC = [0, 384, 2048]
-C0 = [0, 1024, 2048]
-C2 = [0, 1536, 2048]
-ORDER = ["d2", "d0", "s1", "iw", "d0", "d2", "s2", "d1"]
-DPOS = 2
-TAIL = "u0 d0 a0 u1 a1 u2 b3 a2 b2 u3 b1 A3 b0"
+W3 = CAP + 4
+MS = 768
+EARLY = 1
+C2 = [2048, 1664, 1024, 0]
+L2 = [2048, 1664, 1024, 0]
+JC = [0, 576, 1088, 2048]
+RC = [0, 1408, 2048]
+Y0 = [0, 256, 768, 1408, 2048]
+Y1 = [0, 512, 1024, 1536, 2048]
+LOADS = "d20 s1 d21 d22 iw d0 s2 d1"
+VEC = ("fz m2 m0 hu xm2 g20 op t1 t2 g21 t3 t4 g22 js0 js1 js2 jp0 xm0 oa c0 e1 fx e2 xd e3 h0 h1 h2 g1 r1 tm oi rf vv red ss z0 "
+       "u0 dd n0 u1 b3 n1 u2 b2 u3 b1 b0")
+ACT = "w0 w1 w2 p0 p1 p2 cw jp1 x0 x1 x2 jp2 r0 v0 v1 v2 q3 q2 q1 q0 n2 n3"
+POOL = "kz tr jj0 m0 jj1 jj2 tq kn ex2 ex1 kp d1 z0 ex3"
+STORES = "n0 b3 n1 b2 n2 b1 n3 b0"
 
 SCRATCH = {
     "d0": ("sbuf", [128, n], "bfloat16"), "d2": ("sbuf", [128, n], "bfloat16"), "d1": ("sbuf", [128, n + 16], "bfloat16"),
     "m0": ("sbuf", [128, n + 16], "bfloat16"), "m2": ("sbuf", [128, n + 16], "bfloat16"), "z0": ("sbuf", [128, n + 16], "bfloat16"),
-    "kz": ("sbuf", [128, 16], "bfloat16"), "kn": ("sbuf", [128, 16], "bfloat16"), "kp": ("sbuf", [128, 16], "bfloat16"),
+    "kz": ("sbuf", [128, 32], "bfloat16"), "kn": ("sbuf", [128, 16], "bfloat16"), "kp": ("sbuf", [128, 16], "bfloat16"),
     "hd": ("sbuf", [128, 3], "int32"), "hu": ("sbuf", [128, 6], "uint16"),
     "la": ("sbuf", [128, SL + 256], "int32"), "lb": ("sbuf", [128, SL], "int32"),
     "tr": ("sbuf", [128, SL], "int32"), "tq": ("sbuf", [128, SL], "int32"),
-    "pa": ("sbuf", [128, 128], "int32"), "pb": ("sbuf", [128, SL], "int32"), "pc": ("sbuf", [128, SL], "int32"),
-    "oa": ("sbuf", [128, SL + 256], "uint16"), "ob": ("sbuf", [128, 128], "uint16"), "oc": ("sbuf", [128, SL], "uint16"),
-    "od": ("sbuf", [128, SL], "uint16"), "oi": ("sbuf", [128, 208], "uint16"),
+    "pa": ("sbuf", [128, SL + 128], "int32"), "pc": ("sbuf", [128, SL], "int32"),
+    "oa": ("sbuf", [128, SL + 256], "uint16"), "ob": ("sbuf", [128, SL + 128], "uint16"), "oc": ("sbuf", [128, SL], "uint16"),
+    "oi": ("sbuf", [128, 208], "uint16"),
     "cw": ("sbuf", [128, n + N * CAP], "float32"), "sb1": ("sbuf", [128, (N - 1) * CAP], "float32"),
     "g2": ("sbuf", [128, n], "float32"), "w2": ("sbuf", [128, SP + n + N * CAP], "float32"), "r2": ("sbuf", [128, (N - 1) * CAP], "float32"),
     "rr": ("sbuf", [128, n], "float32"), "ss": ("sbuf", [128, n], "float32"), "gp": ("psum", [128, n], "float32"),
-    "vw": ("sbuf", [128, n + N * CAP], "float32"), "sb3": ("sbuf", [128, (N - 1) * CAP], "float32"),
-    "iw": ("sbuf", [128, 4096 + SP], "float32"), "jj": ("sbuf", [128, n + (N - 1) * CAP], "float32"),
+    "vw": ("sbuf", [128, n + 2 * (N - 1) * W3], "float32"),
+    "iw": ("sbuf", [128, 4096 + SP], "float32"), "jj": ("sbuf", [128, n], "float32"),
     "fz": ("sbuf", [128, CAP], "float32"), "it": ("sbuf", [128, 256], "float32"),
     "uu": ("sbuf", [128, n], "float32"), "a0": ("sbuf", [128, n], "float32"), "y0": ("sbuf", [128, n], "float32"),
-    "fx": ("sbuf", [128, 16], "float32"), "tm": ("sbuf", [128, 16], "float32"),
-    "dq": ("sbuf", [128, 4 * N], "float32"), "dc": ("sbuf", [128, 4], "float32"),
+    "fx": ("sbuf", [128, 16], "float32"), "tm": ("sbuf", [128, 16], "float32"), "dc": ("sbuf", [128, 4], "float32"),
 }
-SEMAPHORES = ["a1", "a20", "a21", "a22", "a3", "a4", "sent"] + ["e%d" % k for k in range(135)]
+SEMAPHORES = ["a1", "a20", "a21", "a22", "a3", "sent"] + ["e%d" % k for k in range(140)]
 
 
 def rank_program(g, core, T, topo):
@@ -48,36 +53,34 @@ def rank_program(g, core, T, topo):
     turn = [(r + 1 + k) % N for k in range(N - 1)]
     frm = [(r - 1 - k) % N for k in range(N - 1)]
     V, A, S = g.vector, g.scalar, g.sync
-    nxt = [0]
-    seen = {}
-    made = []
-    sent = [0]
-
-    def ev(ins, k=1):
-        name = "e%d" % nxt[0]
-        nxt[0] += 1
-        ins.then_inc(T.sem[name], k)
-        made.append((name, k))
-        return (name, k)
-
-    def wait(q, qn, *evs):
-        for e in evs:
-            if (qn, e) not in seen:
-                seen[(qn, e)] = True
-                seen[e] = True
-                q.wait_ge(T.sem[e[0]], e[1])
-
-    def vw(*e): wait(V, "v", *e)
-    def aw(*e): wait(A, "a", *e)
-    def sw(*e): wait(S, "s", *e)
-    def gw(*e): wait(g, "g", *e)
+    sems, waited, seen, sent = {}, set(), set(), [0]
+    out = n + (N - 1) * W3
+    D = T.dc[:, 0:1]
+    h = n // 2
 
     def engines(p, q):
         return len(topo.engines(cores[p], cores[q]))
+    count = {"a1": sum(engines(q, r) for q in frm), "a3": sum(engines(q, r) for q in frm + frm[:EARLY])}
+    count.update({"a2%d" % k: engines(q, r) for k, q in enumerate(frm)})
 
-    def send(q, dst, src, sem):
+    def sem(name):
+        if name in count:
+            return T.sem[name], count[name]
+        return T.sem[sems.setdefault(name, "e%d" % len(sems))], 16 if name.startswith("l_") else 1
+
+    def done(name, ins):
+        ins.then_inc(*sem(name))
+
+    def wait(qn, *names):
+        for e in names:
+            if (qn, e) not in seen:
+                seen.add((qn, e))
+                waited.add(e)
+                {"v": V, "a": A, "s": S, "g": g}[qn].wait_ge(*sem(e))
+
+    def send(q, dst, src, name):
         rid, pid, _ = topo.addr(cores[q])
-        g.remote_dma(dst, src, T.sem[sem], T.sem.sent, pid, rid, topo.mask(core, cores[q]))
+        g.remote_dma(dst, src, T.sem[name], T.sem.sent, pid, rid, topo.mask(core, cores[q]))
         sent[0] += engines(r, q)
 
     def slot(t, k, base=0):
@@ -86,238 +89,230 @@ def rank_program(g, core, T, topo):
     def cols(t, q, base=0):
         return t[:, base + q * LC:base + (q + 1) * LC]
 
-    l_hd = ev(A.dma_start(T.hd[:], T.heads[:]), 16)
-    l_pv = ev(A.dma_start(T.la[:, SL:SL + 256], T.prev[:]), 16)
-    f_fz = ev(V.memset(T.fz[:], float(JB)))
-    f_m2 = ev(V.memset(T.m2[:], 1.0))
-    l_d0, l_d2, ld = [], [], {}
-    for w in ORDER:
-        if w == "d0":
-            k = len(l_d0)
-            l_d0.append(ev(S.dma_start(T.d0[:, C0[k]:C0[k + 1]], T.dur[:, C0[k]:C0[k + 1]]), 16))
-        elif w == "d2":
-            k = len(C2) - 2 - len(l_d2)
-            l_d2.append(ev(S.dma_start(T.d2[:, C2[k]:C2[k + 1]], T.dur[:, 2 * n + C2[k]:2 * n + C2[k + 1]]), 16))
-        elif w == "iw":
-            sw(f_fz)
-            ld[w] = ev(S.dma_start(T.iw[::16, 0:4096], T.fz[:, 0:256]), 16)
-        elif w == "s1":
-            ld[w] = ev(S.dma_start(T.la[:, 0:SL], T.ship[:, 0:SL]), 16)
-        elif w == "s2":
-            ld[w] = ev(S.dma_start(T.lb[:], T.ship[:, SL:2 * SL]), 16)
+    def back(lo, hi):
+        return slice(hi - 1, lo - 1 if lo else None, -1)
+
+    def pieces(name, cuts):
+        return [name + str(k) for k in range(len(cuts) - 1)]
+
+    def const(ap, v):
+        return g.iota(ap, [[0, ap.shape[1]]], v, 0, allow_small_or_imprecise_dtypes=True)
+
+    head0, head1, head2 = T.hu[:, 0:1], T.hu[:, 2:3], T.hu[:, 4:5]
+    d1 = T.d1[:, 16:16 + n]
+    order = [w for w in (VEC + " " + ACT).split() if w[:2] in ("js", "jp")]
+
+    def gather(q, dst, win, bias=0.0):
+        if q == "a":
+            return A.activation(dst, win, Fn.Identity, bias=bias)
+        return V.tensor_scalar(dst, win, bias, None, Op.add)
+
+    def call(q, w):
+        k = int(w[-1]) if w[-1].isdigit() else 0
+        a = w.rstrip("0123456789") if w not in ("m0", "m2", "xm0", "xm2", "c0", "g1", "z0", "d1") else w
+        if w.startswith("g2"):
+            a = "g2"
+
+        def after(*names):
+            wait(q, *names)
+        if a == "fz":
+            return V.memset(T.fz[:], float(JB))
+        if a == "m2":
+            return V.memset(T.m2[:], BIG)
+        if a == "m0":
+            return V.memset(T.m0[:, 0:MS], 1.0) if q == "v" else const(T.m0[:, MS:], 1)
+        if a == "z0":
+            if q == "g":
+                return const(T.z0[:], 0)
+            after("gz0", "kp", "hu")
+            return V.tensor_copy(T.z0[:, 0:n].indirect(head0), T.kp[:])
+        if a == "kz":
+            return g.iota(T.kz[:], [[JB, 2], [0, 16]], 0, 0, allow_small_or_imprecise_dtypes=True)
+        if a == "kn":
+            return const(T.kn[:], -int(BIG))
+        if a == "kp":
+            return const(T.kp[:], int(BIG))
+        if a == "d1":
+            return const(T.d1[:, 0:16], 0)
+        if a == "tr":
+            return g.iota(T.tr[:], [[16, SL]], 4096, 1)
+        if a == "tq":
+            return g.iota(T.tq[:], [[16, SL]], 1, 1)
+        if a == "jj":
+            return g.iota(T.jj[:, JC[k]:JC[k + 1]], [[1, JC[k + 1] - JC[k]]], JB + JC[k], 0, allow_small_or_imprecise_dtypes=True)
+        if a == "w":
+            after("fz")
+            return A.activation(slot(T.w2, turn[k], SP + n), T.fz[:], Fn.Silu)
+        if a == "cw":
+            after("fz")
+            return A.activation(slot(T.cw, r, n), T.fz[:], Fn.Identity)
+        if a == "hu":
+            after("l_hd")
+            return V.tensor_copy(T.hu[:, 0:6:2], T.hd[:])
+        if a == "xm2":
+            after("hu", "m2", "kz")
+            return V.tensor_copy(T.m2[:, 0:n].indirect(head2), T.kz[:, 16:32])
+        if a == "xm0":
+            after("hu", "m0", "gm0", "kz")
+            return V.tensor_copy(T.m0[:, 0:n].indirect(head0), T.kz[:, 0:16])
+        if a == "op":
+            after("l_pv")
+            return V.tensor_copy(T.oa[:, SL + 128:], T.la[:, SL + 128:])
+        if a == "oa":
+            after("l_pv", "l_s1")
+            return V.tensor_copy(T.oa[:, 0:SL + 128], T.la[:, 0:SL + 128])
+        if a == "t":
+            after(*([["l_pv", "l_s1"], ["t1"], ["t2", "tr"], ["t3"]][k - 1]))
+            if k == 1:
+                return V.tensor_scalar(T.pa[:], T.la[:, 0:SL + 128], 4097, None, Op.mult)
+            if k == 2:
+                return V.tensor_scalar(T.pa[:], T.pa[:], 4, 0x100FFF, Op.arith_shift_right, Op.bitwise_and)
+            if k == 3:
+                return V.tensor_tensor(T.pa[:, 0:SL], T.pa[:, 0:SL], T.tr[:], Op.min)
+            return V.tensor_copy(T.ob[:], T.pa[:])
+        if a == "e":
+            after(*([["l_s2", "tq"], ["e1"], ["e2"]][k - 1]))
+            if k == 1:
+                return V.tensor_tensor(T.pc[:], T.lb[:], T.tq[:], Op.mult)
+            if k == 2:
+                return V.tensor_tensor(T.pc[:], T.pc[:], T.lb[:], Op.min)
+            return V.tensor_scalar(T.oc[:], T.pc[:], SP, None, Op.add)
+        if a in ("js", "jp"):
+            at = order.index(w)
+            after("t4", order[at - 1] if at else "l_iw")
+            if a == "js":
+                after("jj0")
+                return V.tensor_scalar(T.iw[:].indirect(cols(T.ob, frm[k])), T.jj[:, 0:CAP], 1.0, float(n + k * W3), Op.mult, Op.add)
+            after("jj%d" % k)
+            win, src = T.iw[:].indirect(T.ob[:, SL + JC[k] // 16:SL + JC[k + 1] // 16]), T.jj[:, JC[k]:JC[k + 1]]
+            return V.tensor_copy(win, src) if q == "v" else A.activation(win, src, Fn.Silu)
+        if a == "oi":
+            after("l_it")
+            return V.tensor_scalar(T.oi[:], T.it[:, 0:208], 0.25 - JB, None, Op.add)
+        if a == "c0":
+            after("l_d0", "xm0")
+            return V.tensor_tensor_scan(T.cw[:, 0:n], T.m0[:, 0:n], T.d0[:], 0.0, Op.mult, Op.add)
+        if a == "x":
+            after("oa", "c0")
+            return gather(q, slot(T.sb1, k), T.cw[:, 0:n].indirect(cols(T.oa, turn[k])))
+        if a == "r":
+            after("a1", "cw", "oa", "c0")
+            return gather(q, T.rr[:, RC[k]:RC[k + 1]], T.cw[:].indirect(T.oa[:, SL + RC[k] // 16:SL + RC[k + 1] // 16]), RND)
+        if a == "g2":
+            hi, lo = C2[k], C2[k + 1]
+            after("xm2", *["l_d2%d" % j for j in range(len(L2) - 1) if L2[j] > lo])
+            if k:
+                after("g2%d" % (k - 1))
+            return V.tensor_tensor_scan(T.g2[:, back(lo, hi)], T.m2[:, hi:lo:-1], T.d2[:, back(lo, hi)],
+                                        T.g2[:, hi:hi + 1] if k else float(JB), Op.min, Op.add)
+        if a == "p":
+            hi, lo = C2[k], C2[k + 1]
+            after("op", "g2%d" % k, "p%d" % (k - 1) if k else "w%d" % (N - 2))
+            return A.activation(T.w2[:, SP:].indirect(T.oa[:, SL + 128 + lo // 16:SL + 128 + hi // 16]), T.g2[:, lo:hi], Fn.Silu)
+        if a == "h":
+            after("a2%d" % k, "e3", "h%d" % (k - 1) if k else pieces("p", C2)[-1])
+            return V.tensor_copy(T.w2[:, 0:SP + n].indirect(cols(T.oc, frm[k])), slot(T.r2, k))
+        if a == "fx":
+            after("l_d1", "hu")
+            return V.tensor_scalar(T.fx[:], d1.indirect(head1), BIG, None, Op.add)
+        if a == "xd":
+            after("fx", "kn")
+            return V.tensor_copy(d1.indirect(head1), T.kn[:])
+        if a == "g1":
+            after("h%d" % (N - 2), "xd")
+            return V.tensor_tensor_scan(T.gp[:, ::-1], T.w2[:, SP + n - 1:SP - 1:-1], T.d1[:, n + 15:15:-1], 0.0, Op.max, Op.add)
+        if a == "tm":
+            after("fx", *pieces("r", RC))
+            return V.tensor_tensor(T.tm[:], T.rr[:].indirect(head1), T.fx[:], Op.add)
+        if a == "rf":
+            after("tm")
+            return V.tensor_copy(T.rr[:].indirect(head1), T.tm[:])
+        if a == "vv":
+            after("g1", "rf")
+            return V.tensor_tensor(T.vw[:, 0:n], T.gp[:], T.rr[:], Op.add)
+        if a == "red":
+            after("vv")
+            done("run", V.tensor_tensor_scan(T.y0[:, 0:h], T.vw[:, 0:h], T.vw[:, h:n], 0.0, Op.max, Op.max))
+            after("run")
+            for j in range(N - 1):
+                x = V.tensor_scalar(T.vw[:, out + j * W3 + CAP:out + (j + 1) * W3], T.fz[:, 0:4], 0.0, T.y0[:, h - 1:h], Op.mult, Op.add)
+            return x
+        if a == "v":
+            after("vv", "oi")
+            return gather(q, T.vw[:, out + k * W3:out + k * W3 + CAP], T.vw[:, 0:n].indirect(cols(T.oi, turn[k], 128)))
+        if a == "ss":
+            after("rf", "d1")
+            return V.tensor_tensor_scan(T.ss[:], T.d1[:, 15:15 + n], T.rr[:], 0.0, Op.add, Op.max)
+        if a == "dd":
+            after("a3", "red", "v0")
+            return V.tensor_reduce(D, T.vw[:, n + CAP:out + W3:W3], Ax.X, Op.max)
+        if a == "u":
+            after("ss")
+            return V.tensor_tensor(T.uu[:, Y1[k]:Y1[k + 1]], T.gp[:, Y1[k]:Y1[k + 1]], T.ss[:, Y1[k]:Y1[k + 1]], Op.add)
+        if a == "n":
+            ap = T.uu[:, Y1[k]:Y1[k + 1]]
+            after("u%d" % k, "dd")
+            return V.tensor_scalar(ap, ap, -1.0, D, Op.mult, Op.add) if q == "v" else A.activation(ap, ap, Fn.Identity, bias=D, scale=-1.0)
+        if a == "q":
+            after("a3", "dd", "oi")
+            dst, win = T.a0[:, Y0[k]:Y0[k + 1]], T.vw[:, 0:out].indirect(T.oi[:, Y0[k] // 16:Y0[k + 1] // 16])
+            return V.tensor_scalar(dst, win, -1.0, D, Op.mult, Op.add) if q == "v" else A.activation(dst, win, Fn.Identity, bias=D, scale=-1.0)
+        if a == "b":
+            lo, hi = Y0[k], Y0[k + 1]
+            after("q%d" % k, "z0", "red")
+            if hi < n:
+                after("b%d" % (k + 1))
+            return V.tensor_tensor_scan(T.y0[:, back(lo, hi)], T.z0[:, hi:lo:-1], T.a0[:, back(lo, hi)],
+                                        T.y0[:, hi:hi + 1] if hi < n else BIG, Op.max, Op.min)
+        raise ValueError(w)
+
+    def exchange(k):
+        for j, q in enumerate(turn):
+            if k == 1:
+                wait("g", "x%d" % j)
+                send(q, slot(T.cw, r, n), slot(T.sb1, j), "a1")
+            elif k == 2:
+                wait("g", pieces("p", C2)[-1])
+                send(q, slot(T.r2, j), slot(T.w2, q, SP + n), "a2%d" % j)
+            else:
+                wait("g", "v%d" % j, *(["red"] if j >= EARLY else []))
+                w = CAP if j < EARLY else W3
+                send(q, T.vw[:, n + j * W3:n + j * W3 + w], T.vw[:, out + j * W3:out + j * W3 + w], "a3")
+        for j in range(EARLY if k == 3 else 0):
+            wait("g", "red")
+            send(turn[j], T.vw[:, n + j * W3 + CAP:n + (j + 1) * W3], T.vw[:, out + j * W3 + CAP:out + (j + 1) * W3], "a3")
+
+    done("l_hd", A.dma_start(T.hd[:], T.heads[:]))
+    done("l_pv", A.dma_start(T.la[:, SL:], T.prev[:]))
+    for w in LOADS.split():
+        if w == "iw":
+            wait("s", "fz")
+            x = S.dma_start(T.iw[::16, 0:4096], T.fz[:, 0:256])
+        elif w[:2] == "d2":
+            hi, lo = L2[int(w[2])], L2[int(w[2]) + 1]
+            x = S.dma_start(T.d2[:, lo:hi], T.dur[:, 2 * n + lo:2 * n + hi])
+        elif w[0] == "s":
+            x = S.dma_start(T.la[:, 0:SL], T.ship[:, 0:SL]) if w == "s1" else S.dma_start(T.lb[:], T.ship[:, SL:])
         else:
-            ld[w] = ev(S.dma_start(T.d1[:, 16:16 + n], T.dur[:, n:2 * n]), 16)
-
-    def const(ap, k, v):
-        return ev(g.iota(ap, [[0, k]], v, 0, allow_small_or_imprecise_dtypes=True))
-
-    def count(lo, hi, base):
-        return ev(g.iota(T.jj[:, lo:hi], [[1, hi - lo]], base, 0, allow_small_or_imprecise_dtypes=True))
-    f_kz = const(T.kz[:], 16, 0)
-    f_j = [count(JC[k], JC[k + 1], JB + JC[k]) for k in range(len(JC) - 1)]
-    f_tr = ev(g.iota(T.tr[:], [[16, SL]], 4096, 1))
-    f_tq = ev(g.iota(T.tq[:], [[16, SL]], 4096 - SP, 1))
-    f_kn = const(T.kn[:], 16, -int(BIG))
-
-    aw(f_fz)
-    f_w2 = [ev(A.activation(slot(T.w2, q, SP + n), T.fz[:], Fn.Identity)) for q in turn]
-    f_cw = ev(A.activation(slot(T.cw, r, n), T.fz[:], Fn.Identity))
-
-    g2, sc2 = [], []
-
-    def span2(k):
-        return C2[-2 - k], C2[-1 - k]
-
-    def scan2(k):
-        lo, hi = span2(k)
-        rev = slice(hi - 1, lo - 1 if lo else None, -1)
-        vw(l_d2[k], x_m2, *g2[-1:])
-        g2.append(ev(V.tensor_tensor_scan(T.g2[:, rev], T.m2[:, hi:lo:-1], T.d2[:, rev], T.g2[:, hi:hi + 1] if k else 0.0, Op.mult, Op.add)))
-
-    def scatter2(k):
-        lo, hi = span2(k)
-        vw(x_op, g2[k], *f_w2, *sc2[-1:])
-        sc2.append(ev(V.tensor_copy(T.w2[:, SP:SP + n + N * CAP].indirect(T.oa[:, SL + 128 + lo // 16:SL + 128 + hi // 16]), T.g2[:, lo:hi])))
-
-    vw(l_hd)
-    x_hu = ev(V.tensor_copy(T.hu[:, 0:6:2], T.hd[:]))
-    vw(x_hu, f_m2, f_kz)
-    x_m2 = ev(V.tensor_copy(T.m2[:, 0:n].indirect(T.hu[:, 4:5]), T.kz[:]))
-    aw(x_m2)
-    f_m0 = ev(A.activation(T.m0[:], T.m2[:], Fn.Identity, bias=1.0, scale=0.0))
-    scan2(0)
-    vw(l_pv)
-    x = ev(V.tensor_scalar(T.pa[:], T.la[:, SL:SL + 128], 4097, None, Op.mult))
-    x_op = ev(V.tensor_copy(T.oa[:, SL:SL + 256], T.la[:, SL:SL + 256]))
-    vw(x)
-    x = ev(V.tensor_scalar(T.pa[:], T.pa[:], 4, 0xFFF, Op.arith_shift_right, Op.bitwise_and))
-    vw(x)
-    x_ob = ev(V.tensor_copy(T.ob[:], T.pa[:]))
-    scatter2(0)
-    vw(f_m0)
-    x_m0 = ev(V.tensor_copy(T.m0[:, 0:n].indirect(T.hu[:, 0:1]), T.kz[:]))
-    vw(ld["s1"])
-    x_oa = ev(V.tensor_copy(T.oa[:, 0:SL], T.la[:, 0:SL]))
-    c0 = []
-    vw(x_m0)
-    for k in range(len(C0) - 1):
-        lo, hi = C0[k], C0[k + 1]
-        vw(l_d0[k], *c0[-1:])
-        c0.append(ev(V.tensor_tensor_scan(T.cw[:, lo:hi], T.m0[:, lo:hi], T.d0[:, lo:hi], T.cw[:, lo - 1:lo] if k else 0.0, Op.mult, Op.add)))
-    for k in range(1, len(C2) - 1):
-        scan2(k)
-        scatter2(k)
-    sc2 = sc2[-1]
-
-    last = [ld["iw"]]
-
-    def index_scatter(off, src, *ready):
-        aw(last[0], *ready)
-        last[0] = ev(A.activation(T.iw[:].indirect(off), src, Fn.Silu))
-
-    def prev_piece(k):
-        index_scatter(T.ob[:, JC[k] // 16:JC[k + 1] // 16], T.jj[:, JC[k]:JC[k + 1]], x_ob, f_j[k])
-
-    prev_piece(0)
-    aw(x_oa, *c0)
-    for k, q in enumerate(turn):
-        gw(ev(A.activation(slot(T.sb1, k), T.cw[:, 0:n].indirect(cols(T.oa, q)), Fn.Identity)))
-        send(q, slot(T.cw, r, n), slot(T.sb1, k), "a1")
-    a1 = ("a1", sum(engines(q, r) for q in frm))
-    f_js = count(n, n + (N - 1) * CAP, JB + n)
-    for k in range(1, len(JC) - 1):
-        prev_piece(k)
-
-    gw(sc2)
-    for k, q in enumerate(turn):
-        send(q, slot(T.r2, k), slot(T.w2, q, SP + n), "a2%d" % k)
-    f_kp = const(T.kp[:], 16, int(BIG))
-    f_d1 = const(T.d1[:, 0:16], 16, 0)
-    f_z0 = const(T.z0[:], n + 16, 0)
-
-    x1 = ev(V.tensor_scalar(T.pb[:], T.la[:, 0:SL], 4097, None, Op.mult))
-    vw(ld["s2"])
-    x2 = ev(V.tensor_scalar(T.pc[:], T.lb[:], 4096, None, Op.mult))
-    vw(x1)
-    x1 = ev(V.tensor_scalar(T.pb[:], T.pb[:], 4, 0x100FFF, Op.arith_shift_right, Op.bitwise_and))
-    vw(x2, f_tq)
-    x2 = ev(V.tensor_tensor(T.pc[:], T.pc[:], T.tq[:], Op.add))
-    vw(x1, f_tr)
-    x1 = ev(V.tensor_tensor(T.pb[:], T.pb[:], T.tr[:], Op.min))
-    vw(ld["d1"])
-    fx = ev(V.tensor_scalar(T.fx[:], T.d1[:, 16:16 + n].indirect(T.hu[:, 2:3]), BIG, None, Op.add))
-    vw(x1)
-    x_od = ev(V.tensor_copy(T.od[:], T.pb[:]))
-    vw(x2)
-    x2 = ev(V.tensor_tensor(T.pc[:], T.pc[:], T.lb[:], Op.min))
-    vw(fx, f_kn)
-    x_d1 = ev(V.tensor_copy(T.d1[:, 16:16 + n].indirect(T.hu[:, 2:3]), T.kn[:]))
-    vw(x2)
-    x_oc = ev(V.tensor_scalar(T.oc[:], T.pc[:], SP, None, Op.add))
-    RA = n - RD
-    rs = []
-    if RD:
-        vw(a1, f_cw)
-        rs.append(ev(V.tensor_copy(T.rr[:, RA:n], T.cw[:].indirect(T.oa[:, SL + RA // 16:SL + 128]))))
-
-    for k, q in enumerate(frm):
-        index_scatter(cols(T.od, q), slot(T.jj, k, n), x_od, f_js)
-    aw(a1, f_cw, x_op)
-    rs.append(ev(A.activation(T.rr[:, 0:RA], T.cw[:].indirect(T.oa[:, SL:SL + RA // 16]), Fn.Identity)))
-    sw(last[0])
-    l_it = ev(S.dma_start(T.it[:], T.iw[::16, 0:4096]), 16)
-
-    sh2 = sc2
-    for k, q in enumerate(frm):
-        vw(("a2%d" % k, engines(q, r)), sh2, x_oc)
-        sh2 = ev(V.tensor_copy(T.w2[:, 0:SP + n].indirect(cols(T.oc, q)), slot(T.r2, k)))
-    vw(sh2, x_d1)
-    g1 = ev(V.tensor_tensor_scan(T.gp[:, ::-1], T.w2[:, SP + n - 1:SP - 1:-1], T.d1[:, n + 15:15:-1], 0.0, Op.max, Op.add))
-    vw(*rs)
-    x = ev(V.tensor_tensor(T.tm[:], T.rr[:].indirect(T.hu[:, 2:3]), T.fx[:], Op.add))
-    vw(l_it)
-    x_oi = ev(V.tensor_scalar(T.oi[:], T.it[:, 0:208], 0.25 - JB, None, Op.add))
-    vw(x)
-    rfix = ev(V.tensor_copy(T.rr[:].indirect(T.hu[:, 2:3]), T.tm[:]))
-    vw(g1, rfix)
-    vv = ev(V.tensor_tensor(T.vw[:, 0:n], T.gp[:], T.rr[:], Op.add))
-    mine = T.dq[:, 4 * r:4 * r + 1]
-    vw(vv)
-    red = ev(V.tensor_reduce(mine, T.vw[:, 0:n], Ax.X, Op.max))
-
-    aw(vv, x_oi)
-    ids = [DstId(rid=topo.addr(cores[q])[0], pnc=topo.addr(cores[q])[1]) for q in turn]
-
-    def send_max():
-        gw(red)
-        g.remote_dma_fused([RemoteDMATransfer(dst_ids=ids, dma_engine_mask=topo.mask(core, cores[turn[0]]), remote_sem=T.sem.a4,
-                                              srcs=[mine], dsts=[mine for p in turn])], local_sem=T.sem.sent)
-        sent[0] += engines(r, turn[0])
-    for k, q in enumerate(turn):
-        e = ev(A.activation(slot(T.sb3, k), T.vw[:, 0:n].indirect(cols(T.oi, q, 128)), Fn.Identity))
-        if k == DPOS:
-            send_max()
-        gw(e)
-        send(q, slot(T.vw, k, n), slot(T.sb3, k), "a3")
-    if DPOS >= N - 1:
-        send_max()
-    a3 = ("a3", sum(engines(q, r) for q in frm))
-    a4 = ("a4", sum(engines(q, (q + 1) % N) for q in frm))
-
-    vw(f_d1)
-    ss = ev(V.tensor_tensor_scan(T.ss[:], T.d1[:, 15:15 + n], T.rr[:], 0.0, Op.add, Op.max))
-    vw(f_z0, f_kp)
-    x_z0 = ev(V.tensor_copy(T.z0[:, 0:n].indirect(T.hu[:, 0:1]), T.kp[:]))
-    us, ga, sc, dd = {}, {}, {}, []
-    D = T.dc[:, 0:1]
-
-    def u_piece(k):
-        vw(ss)
-        us[k] = ev(V.tensor_tensor(T.uu[:, k * CH:(k + 1) * CH], T.gp[:, k * CH:(k + 1) * CH], T.ss[:, k * CH:(k + 1) * CH], Op.add))
-
-    def d_piece():
-        vw(a4, red)
-        dd.append(ev(V.tensor_reduce(D, T.dq[:, ::4], Ax.X, Op.max)))
-        aw(a3, *dd)
-        for k in range(NCH - 1, -1, -1):
-            ga[k] = ev(A.activation(T.a0[:, k * CH:(k + 1) * CH],
-                                    T.vw[:, 0:n + (N - 1) * CAP].indirect(T.oi[:, k * CH // 16:(k + 1) * CH // 16]),
-                                    Fn.Identity, bias=D, scale=-1.0))
-
-    def store(e, col, src):
-        sw(e)
-        ev(S.dma_start(T.y[:, col:col + CH], src), 16)
-
-    def s1_piece(k, on_v):
-        ap = T.uu[:, k * CH:(k + 1) * CH]
-        if on_v:
-            vw(us[k], *dd)
-            e = ev(V.tensor_scalar(ap, ap, -1.0, D, Op.mult, Op.add))
+            x = S.dma_start(T.d0[:], T.dur[:, 0:n]) if w == "d0" else S.dma_start(d1, T.dur[:, n:2 * n])
+        done("l_" + w, x)
+    for w in VEC.split():
+        done(w, call("v", w))
+    for w in ACT.split():
+        done(w, call("a", w))
+    for w in POOL.split():
+        if w[:2] == "ex":
+            exchange(int(w[2]))
         else:
-            aw(us[k])
-            e = ev(A.activation(ap, ap, Fn.Identity, bias=D, scale=-1.0))
-        store(e, n + k * CH, ap)
-
-    def s0_piece(k):
-        lo, hi = k * CH, (k + 1) * CH
-        rev = slice(hi - 1, lo - 1 if lo else None, -1)
-        vw(ga[k], x_z0)
-        if k < NCH - 1:
-            vw(sc[k + 1])
-        sc[k] = ev(V.tensor_tensor_scan(T.y0[:, rev], T.z0[:, hi:lo:-1], T.a0[:, rev],
-                                        BIG if k == NCH - 1 else T.y0[:, hi:hi + 1], Op.max, Op.min))
-        store(sc[k], lo, T.y0[:, lo:hi])
-
-    for w in TAIL.split():
-        k = int(w[1:])
-        if w[0] == "u":
-            u_piece(k)
-        elif w[0] == "d":
-            d_piece()
-        elif w[0] == "b":
-            s0_piece(k)
+            done("g" + w if w in ("m0", "z0") else w, call("g", w))
+    wait("s", order[-1])
+    done("l_it", S.dma_start(T.it[:], T.iw[::16, 0:4096]))
+    for w in STORES.split():
+        k = int(w[1])
+        wait("s", w)
+        if w[0] == "n":
+            done("l_" + w, S.dma_start(T.y[:, n + Y1[k]:n + Y1[k + 1]], T.uu[:, Y1[k]:Y1[k + 1]]))
         else:
-            s1_piece(k, w[0] == "a")
-
-    gw(("sent", sent[0]))
-    sw(*[e for e in made if e not in seen])
+            done("l_" + w, S.dma_start(T.y[:, Y0[k]:Y0[k + 1]], T.y0[:, Y0[k]:Y0[k + 1]]))
+    g.wait_ge(T.sem.sent, sent[0])
+    wait("s", *[e for e in list(sems) if e not in waited])

@@ -1,3 +1,4 @@
+from concourse.bass import DstId, RemoteDMATransfer
 from concourse.mybir import AluOpType as Op, AxisListType as Ax, ActivationFunctionType as Fn
 
 N, n, CAP = 4, 2048, 320
@@ -7,21 +8,21 @@ LC = CAP // 16
 SL = N * LC
 SP = 1392
 JB = 64
-W3 = CAP + 4
-MS = 768
-EARLY = 1
-C2 = [2048, 1664, 1024, 0]
-L2 = [2048, 1664, 1024, 0]
-JC = [0, 576, 1088, 2048]
-RC = [0, 1408, 2048]
-Y0 = [0, 256, 768, 1408, 2048]
-Y1 = [0, 512, 1024, 1536, 2048]
-LOADS = "d20 s1 d21 d22 iw d0 s2 d1"
-VEC = ("fz m2 m0 hu xm2 g20 op t1 t2 g21 t3 t4 g22 js0 js1 js2 jp0 xm0 oa c0 e1 fx e2 xd e3 h0 h1 h2 g1 r1 tm oi rf vv red ss z0 "
-       "u0 dd n0 u1 b3 n1 u2 b2 u3 b1 b0")
-ACT = "w0 w1 w2 p0 p1 p2 cw jp1 x0 x1 x2 jp2 r0 v0 v1 v2 q3 q2 q1 q0 n2 n3"
-POOL = "kz tr jj0 m0 jj1 jj2 tq kn ex2 ex1 kp d1 z0 ex3"
-STORES = "n0 b3 n1 b2 n2 b1 n3 b0"
+BANK = 512
+MS = 1664
+C2 = [2048, 1664, 768, 0]
+L2 = [2048, 1440, 768, 0]
+JC = [0, 1024, 1408, 2048]
+RC = [0, 1984, 2048]
+Y0 = [0, 352, 864, 1440, 2048]
+Y1 = [0, 160, 1024, 1472, 2048]
+LOADS = "d20 d21 s1 d0 d22 s2 iw d1 iv"
+VEC = ("fz m2 m0 hu xm2 g20 op xm0 g21 t1 oa c0 g22 t2 e1 t3 t4 e2 jp0 fx e3 js0 h0 xd h1 h2 r1 g1 tm rf oi vv ss0 red ss1 "
+       "u0 u1 dd z0 om ss2 on u2 ss3 b3 u3 b2 b1 b0")
+ACT = "w0 w1 w2 cw p0 p1 x0 p2 x2 x1 jp2 jp1 r0 js2 js1 v1 v0 v2 n0 n1 q3 n2 q2 q1 q0 n3"
+POOL = "kz tr tq m0 jj2 jq jj0 X0 kn H0 H1 H2 X2 X1 jj1 kp z0 d1 V1 mx V0 V2"
+PEQ = ""
+STORES = "it iu n1 n0 b3 n2 b2 b1 b0 n3"
 
 SCRATCH = {
     "d0": ("sbuf", [128, n], "bfloat16"), "d2": ("sbuf", [128, n], "bfloat16"), "d1": ("sbuf", [128, n + 16], "bfloat16"),
@@ -36,13 +37,14 @@ SCRATCH = {
     "cw": ("sbuf", [128, n + N * CAP], "float32"), "sb1": ("sbuf", [128, (N - 1) * CAP], "float32"),
     "g2": ("sbuf", [128, n], "float32"), "w2": ("sbuf", [128, SP + n + N * CAP], "float32"), "r2": ("sbuf", [128, (N - 1) * CAP], "float32"),
     "rr": ("sbuf", [128, n], "float32"), "ss": ("sbuf", [128, n], "float32"), "gp": ("psum", [128, n], "float32"),
-    "vw": ("sbuf", [128, n + 2 * (N - 1) * W3], "float32"),
-    "iw": ("sbuf", [128, 4096 + SP], "float32"), "jj": ("sbuf", [128, n], "float32"),
-    "fz": ("sbuf", [128, CAP], "float32"), "it": ("sbuf", [128, 256], "float32"),
+    "vw": ("sbuf", [128, n + (N - 1) * CAP], "float32"), "sb3": ("sbuf", [128, (N - 1) * CAP], "float32"),
+    "iw": ("sbuf", [128, 4096], "float32"), "iv": ("sbuf", [128, 4096 + SP], "float32"), "jj": ("sbuf", [128, n + (N - 1) * CAP], "float32"),
+    "fz": ("sbuf", [128, CAP], "float32"), "it": ("sbuf", [128, 256], "float32"), "iu": ("sbuf", [128, 256], "float32"),
     "uu": ("sbuf", [128, n], "float32"), "a0": ("sbuf", [128, n], "float32"), "y0": ("sbuf", [128, n], "float32"),
     "fx": ("sbuf", [128, 16], "float32"), "tm": ("sbuf", [128, 16], "float32"), "dc": ("sbuf", [128, 4], "float32"),
+    "dq": ("sbuf", [128, 4 * N], "float32"), "on": ("sbuf", [128, 128], "float32"), "ey": ("sbuf", [128, 128], "float32"),
 }
-SEMAPHORES = ["a1", "a20", "a21", "a22", "a3", "sent"] + ["e%d" % k for k in range(140)]
+SEMAPHORES = ["a1", "a20", "a21", "a22", "a3", "a4", "sent"] + ["e%d" % k for k in range(140)]
 
 
 def rank_program(g, core, T, topo):
@@ -52,15 +54,14 @@ def rank_program(g, core, T, topo):
     cores = list(T.cores)
     turn = [(r + 1 + k) % N for k in range(N - 1)]
     frm = [(r - 1 - k) % N for k in range(N - 1)]
-    V, A, S = g.vector, g.scalar, g.sync
+    V, A, S, P = g.vector, g.scalar, g.sync, g.tensor
     sems, waited, seen, sent = {}, set(), set(), [0]
-    out = n + (N - 1) * W3
     D = T.dc[:, 0:1]
     h = n // 2
 
     def engines(p, q):
         return len(topo.engines(cores[p], cores[q]))
-    count = {"a1": sum(engines(q, r) for q in frm), "a3": sum(engines(q, r) for q in frm + frm[:EARLY])}
+    count = {a: sum(engines(q, r) for q in frm) for a in ("a1", "a3", "a4")}
     count.update({"a2%d" % k: engines(q, r) for k, q in enumerate(frm)})
 
     def sem(name):
@@ -76,12 +77,7 @@ def rank_program(g, core, T, topo):
             if (qn, e) not in seen:
                 seen.add((qn, e))
                 waited.add(e)
-                {"v": V, "a": A, "s": S, "g": g}[qn].wait_ge(*sem(e))
-
-    def send(q, dst, src, name):
-        rid, pid, _ = topo.addr(cores[q])
-        g.remote_dma(dst, src, T.sem[name], T.sem.sent, pid, rid, topo.mask(core, cores[q]))
-        sent[0] += engines(r, q)
+                {"v": V, "a": A, "s": S, "g": g, "p": P}[qn].wait_ge(*sem(e))
 
     def slot(t, k, base=0):
         return t[:, base + k * CAP:base + (k + 1) * CAP]
@@ -98,14 +94,24 @@ def rank_program(g, core, T, topo):
     def const(ap, v):
         return g.iota(ap, [[0, ap.shape[1]]], v, 0, allow_small_or_imprecise_dtypes=True)
 
+    def count_up(lo, hi):
+        return g.iota(T.jj[:, lo:hi], [[1, hi - lo]], JB + lo, 0, allow_small_or_imprecise_dtypes=True)
+
     head0, head1, head2 = T.hu[:, 0:1], T.hu[:, 2:3], T.hu[:, 4:5]
     d1 = T.d1[:, 16:16 + n]
-    order = [w for w in (VEC + " " + ACT).split() if w[:2] in ("js", "jp")]
+    mine = T.dq[:, 4 * r:4 * r + 1]
+    order = {a: [w for w in (VEC + " " + ACT).split() if w[:2] == a] for a in ("js", "jp")}
+    on_pe = PEQ.split()
 
     def gather(q, dst, win, bias=0.0):
         if q == "a":
             return A.activation(dst, win, Fn.Identity, bias=bias)
         return V.tensor_scalar(dst, win, bias, None, Op.add)
+
+    def from_d(q, dst, src):
+        if q == "a":
+            return A.activation(dst, src, Fn.Identity, bias=D, scale=-1.0)
+        return V.tensor_scalar(dst, src, -1.0, D, Op.mult, Op.add)
 
     def call(q, w):
         k = int(w[-1]) if w[-1].isdigit() else 0
@@ -139,7 +145,13 @@ def rank_program(g, core, T, topo):
         if a == "tq":
             return g.iota(T.tq[:], [[16, SL]], 1, 1)
         if a == "jj":
-            return g.iota(T.jj[:, JC[k]:JC[k + 1]], [[1, JC[k + 1] - JC[k]]], JB + JC[k], 0, allow_small_or_imprecise_dtypes=True)
+            return count_up(JC[k], JC[k + 1])
+        if a == "jq":
+            return count_up(n, n + (N - 1) * CAP)
+        if a == "ey":
+            done("ones", const(T.on[:], 1))
+            after("ones")
+            return g.affine_select(T.ey[:], T.on[:], [[-1, 128]], Op.is_equal, 0.0, 0, 1)
         if a == "w":
             after("fz")
             return A.activation(slot(T.w2, turn[k], SP + n), T.fz[:], Fn.Silu)
@@ -178,17 +190,22 @@ def rank_program(g, core, T, topo):
                 return V.tensor_tensor(T.pc[:], T.pc[:], T.lb[:], Op.min)
             return V.tensor_scalar(T.oc[:], T.pc[:], SP, None, Op.add)
         if a in ("js", "jp"):
-            at = order.index(w)
-            after("t4", order[at - 1] if at else "l_iw")
+            at = order[a].index(w)
+            after("t4", order[a][at - 1] if at else "l_iw" if a == "jp" else "l_iv", "jq" if a == "js" else "jj%d" % k)
             if a == "js":
-                after("jj0")
-                return V.tensor_scalar(T.iw[:].indirect(cols(T.ob, frm[k])), T.jj[:, 0:CAP], 1.0, float(n + k * W3), Op.mult, Op.add)
-            after("jj%d" % k)
-            win, src = T.iw[:].indirect(T.ob[:, SL + JC[k] // 16:SL + JC[k + 1] // 16]), T.jj[:, JC[k]:JC[k + 1]]
+                win, src = T.iv[:].indirect(cols(T.ob, frm[k])), slot(T.jj, k, n)
+            else:
+                win, src = T.iw[:].indirect(T.ob[:, SL + JC[k] // 16:SL + JC[k + 1] // 16]), T.jj[:, JC[k]:JC[k + 1]]
             return V.tensor_copy(win, src) if q == "v" else A.activation(win, src, Fn.Silu)
         if a == "oi":
             after("l_it")
-            return V.tensor_scalar(T.oi[:], T.it[:, 0:208], 0.25 - JB, None, Op.add)
+            return V.tensor_scalar(T.oi[:, 128:], T.it[:, 128:208], 0.25 - JB, None, Op.add)
+        if a == "om":
+            after("l_it", "l_iu")
+            return V.tensor_tensor(T.iu[:, 0:128], T.iu[:, 0:128], T.it[:, 0:128], Op.add)
+        if a == "on":
+            after("om")
+            return V.tensor_scalar(T.oi[:, 0:128], T.iu[:, 0:128], 0.25 - 2 * JB, None, Op.add)
         if a == "c0":
             after("l_d0", "xm0")
             return V.tensor_tensor_scan(T.cw[:, 0:n], T.m0[:, 0:n], T.d0[:], 0.0, Op.mult, Op.add)
@@ -207,7 +224,7 @@ def rank_program(g, core, T, topo):
                                         T.g2[:, hi:hi + 1] if k else float(JB), Op.min, Op.add)
         if a == "p":
             hi, lo = C2[k], C2[k + 1]
-            after("op", "g2%d" % k, "p%d" % (k - 1) if k else "w%d" % (N - 2))
+            after("op", "g2%d" % k, *(["p%d" % (k - 1)] if k else pieces("w", range(N))))
             return A.activation(T.w2[:, SP:].indirect(T.oa[:, SL + 128 + lo // 16:SL + 128 + hi // 16]), T.g2[:, lo:hi], Fn.Silu)
         if a == "h":
             after("a2%d" % k, "e3", "h%d" % (k - 1) if k else pieces("p", C2)[-1])
@@ -218,8 +235,11 @@ def rank_program(g, core, T, topo):
         if a == "xd":
             after("fx", "kn")
             return V.tensor_copy(d1.indirect(head1), T.kn[:])
+        if a == "o":
+            after("xm0")
+            return P.matmul(T.gp[:, k * BANK:(k + 1) * BANK], T.m0[:, 0:128], T.m0[:, 0:BANK], True, False)
         if a == "g1":
-            after("h%d" % (N - 2), "xd")
+            after("h%d" % (N - 2), "xd", *[x for x in on_pe if x[0] == "o"])
             return V.tensor_tensor_scan(T.gp[:, ::-1], T.w2[:, SP + n - 1:SP - 1:-1], T.d1[:, n + 15:15:-1], 0.0, Op.max, Op.add)
         if a == "tm":
             after("fx", *pieces("r", RC))
@@ -234,29 +254,30 @@ def rank_program(g, core, T, topo):
             after("vv")
             done("run", V.tensor_tensor_scan(T.y0[:, 0:h], T.vw[:, 0:h], T.vw[:, h:n], 0.0, Op.max, Op.max))
             after("run")
-            for j in range(N - 1):
-                x = V.tensor_scalar(T.vw[:, out + j * W3 + CAP:out + (j + 1) * W3], T.fz[:, 0:4], 0.0, T.y0[:, h - 1:h], Op.mult, Op.add)
-            return x
+            return V.tensor_copy(mine, T.y0[:, h - 1:h])
         if a == "v":
             after("vv", "oi")
-            return gather(q, T.vw[:, out + k * W3:out + k * W3 + CAP], T.vw[:, 0:n].indirect(cols(T.oi, turn[k], 128)))
+            return gather(q, slot(T.sb3, k), T.vw[:, 0:n].indirect(cols(T.oi, turn[k], 128)))
         if a == "ss":
-            after("rf", "d1")
-            return V.tensor_tensor_scan(T.ss[:], T.d1[:, 15:15 + n], T.rr[:], 0.0, Op.add, Op.max)
+            lo, hi = Y1[k], Y1[k + 1]
+            after("rf", "xd", "d1", *(["ss%d" % (k - 1)] if k else []))
+            return V.tensor_tensor_scan(T.ss[:, lo:hi], T.d1[:, 15 + lo:15 + hi], T.rr[:, lo:hi], T.ss[:, lo - 1:lo] if k else 0.0, Op.add, Op.max)
         if a == "dd":
-            after("a3", "red", "v0")
-            return V.tensor_reduce(D, T.vw[:, n + CAP:out + W3:W3], Ax.X, Op.max)
+            after("red", "a4")
+            return V.tensor_reduce(D, T.dq[:, ::4], Ax.X, Op.max)
         if a == "u":
-            after("ss")
-            return V.tensor_tensor(T.uu[:, Y1[k]:Y1[k + 1]], T.gp[:, Y1[k]:Y1[k + 1]], T.ss[:, Y1[k]:Y1[k + 1]], Op.add)
+            lo, hi = Y1[k], Y1[k + 1]
+            after("ss%d" % k, "g1")
+            if q == "p":
+                after("vv", "ey")
+                return P.matmul(T.gp[:, lo:hi], T.ey[:], T.ss[:, lo:hi], False, True)
+            return V.tensor_tensor(T.uu[:, lo:hi], T.gp[:, lo:hi], T.ss[:, lo:hi], Op.add)
         if a == "n":
-            ap = T.uu[:, Y1[k]:Y1[k + 1]]
             after("u%d" % k, "dd")
-            return V.tensor_scalar(ap, ap, -1.0, D, Op.mult, Op.add) if q == "v" else A.activation(ap, ap, Fn.Identity, bias=D, scale=-1.0)
+            return from_d(q, T.uu[:, Y1[k]:Y1[k + 1]], (T.gp if "u%d" % k in on_pe else T.uu)[:, Y1[k]:Y1[k + 1]])
         if a == "q":
-            after("a3", "dd", "oi")
-            dst, win = T.a0[:, Y0[k]:Y0[k + 1]], T.vw[:, 0:out].indirect(T.oi[:, Y0[k] // 16:Y0[k + 1] // 16])
-            return V.tensor_scalar(dst, win, -1.0, D, Op.mult, Op.add) if q == "v" else A.activation(dst, win, Fn.Identity, bias=D, scale=-1.0)
+            after("a3", "dd", "on")
+            return from_d(q, T.a0[:, Y0[k]:Y0[k + 1]], T.vw[:].indirect(T.oi[:, Y0[k] // 16:Y0[k + 1] // 16]))
         if a == "b":
             lo, hi = Y0[k], Y0[k + 1]
             after("q%d" % k, "z0", "red")
@@ -266,28 +287,30 @@ def rank_program(g, core, T, topo):
                                         T.y0[:, hi:hi + 1] if hi < n else BIG, Op.max, Op.min)
         raise ValueError(w)
 
-    def exchange(k):
-        for j, q in enumerate(turn):
-            if k == 1:
-                wait("g", "x%d" % j)
-                send(q, slot(T.cw, r, n), slot(T.sb1, j), "a1")
-            elif k == 2:
-                wait("g", pieces("p", C2)[-1])
-                send(q, slot(T.r2, j), slot(T.w2, q, SP + n), "a2%d" % j)
-            else:
-                wait("g", "v%d" % j, *(["red"] if j >= EARLY else []))
-                w = CAP if j < EARLY else W3
-                send(q, T.vw[:, n + j * W3:n + j * W3 + w], T.vw[:, out + j * W3:out + j * W3 + w], "a3")
-        for j in range(EARLY if k == 3 else 0):
+    def remote(w):
+        if w == "mx":
             wait("g", "red")
-            send(turn[j], T.vw[:, n + j * W3 + CAP:n + (j + 1) * W3], T.vw[:, out + j * W3 + CAP:out + (j + 1) * W3], "a3")
+            ids = [DstId(rid=topo.addr(cores[q])[0], pnc=topo.addr(cores[q])[1]) for q in turn]
+            g.remote_dma_fused([RemoteDMATransfer(dst_ids=ids, dma_engine_mask=topo.mask(core, cores[turn[0]]), remote_sem=T.sem.a4,
+                                                  srcs=[mine], dsts=[mine for p in turn])], local_sem=T.sem.sent)
+            sent[0] += engines(r, turn[0])
+            return
+        k = int(w[1])
+        q = turn[k]
+        ready, dst, src, name = {"X": ("x%d" % k, slot(T.cw, r, n), slot(T.sb1, k), "a1"),
+                                 "H": (pieces("p", C2)[-1], slot(T.r2, k), slot(T.w2, q, SP + n), "a2%d" % k),
+                                 "V": ("v%d" % k, slot(T.vw, k, n), slot(T.sb3, k), "a3")}[w[0]]
+        wait("g", ready)
+        rid, pid, _ = topo.addr(cores[q])
+        g.remote_dma(dst, src, T.sem[name], T.sem.sent, pid, rid, topo.mask(core, cores[q]))
+        sent[0] += engines(r, q)
 
     done("l_hd", A.dma_start(T.hd[:], T.heads[:]))
     done("l_pv", A.dma_start(T.la[:, SL:], T.prev[:]))
     for w in LOADS.split():
-        if w == "iw":
+        if w[0] == "i":
             wait("s", "fz")
-            x = S.dma_start(T.iw[::16, 0:4096], T.fz[:, 0:256])
+            x = S.dma_start(T[w][::16, 0:4096], T.fz[:, 0:256])
         elif w[:2] == "d2":
             hi, lo = L2[int(w[2])], L2[int(w[2]) + 1]
             x = S.dma_start(T.d2[:, lo:hi], T.dur[:, 2 * n + lo:2 * n + hi])
@@ -296,23 +319,23 @@ def rank_program(g, core, T, topo):
         else:
             x = S.dma_start(T.d0[:], T.dur[:, 0:n]) if w == "d0" else S.dma_start(d1, T.dur[:, n:2 * n])
         done("l_" + w, x)
-    for w in VEC.split():
-        done(w, call("v", w))
-    for w in ACT.split():
-        done(w, call("a", w))
+    for q, names in (("v", VEC), ("a", ACT), ("p", PEQ)):
+        for w in names.split():
+            done(w, call(q, w))
     for w in POOL.split():
-        if w[:2] == "ex":
-            exchange(int(w[2]))
+        if w[0] in "XHV" or w == "mx":
+            remote(w)
         else:
             done("g" + w if w in ("m0", "z0") else w, call("g", w))
-    wait("s", order[-1])
-    done("l_it", S.dma_start(T.it[:], T.iw[::16, 0:4096]))
     for w in STORES.split():
-        k = int(w[1])
-        wait("s", w)
-        if w[0] == "n":
-            done("l_" + w, S.dma_start(T.y[:, n + Y1[k]:n + Y1[k + 1]], T.uu[:, Y1[k]:Y1[k + 1]]))
+        if w[0] == "i":
+            wait("s", order["jp" if w == "it" else "js"][-1])
+            x = S.dma_start(T[w][:], (T.iw if w == "it" else T.iv)[::16, 0:4096])
         else:
-            done("l_" + w, S.dma_start(T.y[:, Y0[k]:Y0[k + 1]], T.y0[:, Y0[k]:Y0[k + 1]]))
+            wait("s", w)
+            cut, src, base = (Y1, T.uu, n) if w[0] == "n" else (Y0, T.y0, 0)
+            lo, hi = cut[int(w[1])], cut[int(w[1]) + 1]
+            x = S.dma_start(T.y[:, base + lo:base + hi], src[:, lo:hi])
+        done("l_" + w, x)
     g.wait_ge(T.sem.sent, sent[0])
     wait("s", *[e for e in list(sems) if e not in waited])

@@ -5,44 +5,51 @@ N, n, CAP = 4, 2048, 320
 BIG = float(1 << 20)
 RND = float(3 << 22)
 LC = CAP // 16
-SL = N * LC
-SP = 1392
+SL = (N - 1) * LC
+SP = 1088
 JB = 64
 BANK = 512
-MS = 1664
-C2 = [2048, 1664, 768, 0]
-L2 = [2048, 1440, 768, 0]
-JC = [0, 1024, 1408, 2048]
-RC = [0, 1984, 2048]
-Y0 = [0, 352, 864, 1440, 2048]
-Y1 = [0, 160, 1024, 1472, 2048]
-LOADS = "d20 d21 s1 d0 d22 s2 iw d1 iv"
-VEC = ("fz m2 m0 hu xm2 g20 op xm0 g21 t1 oa c0 g22 t2 e1 t3 t4 e2 jp0 fx e3 js0 h0 xd h1 h2 r1 g1 tm rf oi vv ss0 red ss1 "
-       "u0 u1 dd z0 om ss2 on u2 ss3 b3 u3 b2 b1 b0")
-ACT = "w0 w1 w2 cw p0 p1 x0 p2 x2 x1 jp2 jp1 r0 js2 js1 v1 v0 v2 n0 n1 q3 n2 q2 q1 q0 n3"
-POOL = "kz tr tq m0 jj2 jq jj0 X0 kn H0 H1 H2 X2 X1 jj1 kp z0 d1 V1 mx V0 V2"
-PEQ = ""
-STORES = "it iu n1 n0 b3 n2 b2 b1 b0 n3"
+HALF = n // 2
+WAW = True
+GS = 1024
+C2 = [2048, 1696, 640, 0]
+L2 = C2
+JC = [0, 832, 2048]
+JJ = [0, 1216]
+RC = [0, 448, 2048]
+VC = [0, 512, 1024, 2048]
+Y0 = [0, 288, 928, 1472, 2048]
+Y1 = [0, 704, 1120, 1760, 2048]
+ZV = 1232
+LOADS = "p2 d20 d21 d0 p1 d22 s1a s1b s2a s2b iv iw da db d1"
+VEC = "fz m2 z0 hu xm2 op g20 xm0 g21 c0 oa g22 t1 e1 t2 xb e2 t3 xa t4 jp1 h2 h01 ga ok gz gb vv2 vv1 vv0 oi red ss0 ss1 u0 ss2 dd om u2 on ss3 q3 u3 b3 b2 b1 b0"
+ACT = "w1 w0 p0 p1 x0 p2 x1 x2 jp0 r1 js2 r0 js01 v1 v0 v2 n0 n1 n2 q2 q1 n3 q0"
+POOL = "w2 zg kp zb tr jj0 kn zf X0 H0 H1 H2 X1 X2 eb jq01 jq2 ef nf mx V1 V0 V2"
+PEQ = "o3 o2 o1 o0 d3 d2 d1 d0 pa1 pb1 pc1"
+STORES = "ik it iu n0 n1 n2 b3 b2 n3 b1 b0"
 
 SCRATCH = {
-    "d0": ("sbuf", [128, n], "bfloat16"), "d2": ("sbuf", [128, n], "bfloat16"), "d1": ("sbuf", [128, n + 16], "bfloat16"),
-    "m0": ("sbuf", [128, n + 16], "bfloat16"), "m2": ("sbuf", [128, n + 16], "bfloat16"), "z0": ("sbuf", [128, n + 16], "bfloat16"),
-    "kz": ("sbuf", [128, 32], "bfloat16"), "kn": ("sbuf", [128, 16], "bfloat16"), "kp": ("sbuf", [128, 16], "bfloat16"),
+    "d0": ("sbuf", [128, n], "bfloat16"), "d2": ("sbuf", [128, n], "bfloat16"), "d1": ("sbuf", [128, n], "bfloat16"),
+    "da": ("sbuf", [128, n + 16], "bfloat16"), "db": ("sbuf", [128, n], "bfloat16"),
+    "zb": ("sbuf", [128, 128], "bfloat16"), "eb": ("sbuf", [128, 128], "bfloat16"),
+    "m2": ("sbuf", [128, n + 16], "bfloat16"), "z0": ("sbuf", [128, n + 16], "bfloat16"),
+    "kn": ("sbuf", [128, 16], "bfloat16"), "kp": ("sbuf", [128, 16], "bfloat16"),
     "hd": ("sbuf", [128, 3], "int32"), "hu": ("sbuf", [128, 6], "uint16"),
-    "la": ("sbuf", [128, SL + 256], "int32"), "lb": ("sbuf", [128, SL], "int32"),
-    "tr": ("sbuf", [128, SL], "int32"), "tq": ("sbuf", [128, SL], "int32"),
-    "pa": ("sbuf", [128, SL + 128], "int32"), "pc": ("sbuf", [128, SL], "int32"),
-    "oa": ("sbuf", [128, SL + 256], "uint16"), "ob": ("sbuf", [128, SL + 128], "uint16"), "oc": ("sbuf", [128, SL], "uint16"),
+    "la": ("sbuf", [128, 256 + 2 * SL], "int32"), "tr": ("sbuf", [128, 2 * SL], "int32"), "pa": ("sbuf", [128, 128 + 2 * SL], "int32"),
+    "op": ("sbuf", [128, 128], "uint16"), "oa": ("sbuf", [128, 128 + SL], "uint16"), "ob": ("sbuf", [128, 128 + 2 * SL], "uint16"),
     "oi": ("sbuf", [128, 208], "uint16"),
     "cw": ("sbuf", [128, n + N * CAP], "float32"), "sb1": ("sbuf", [128, (N - 1) * CAP], "float32"),
     "g2": ("sbuf", [128, n], "float32"), "w2": ("sbuf", [128, SP + n + N * CAP], "float32"), "r2": ("sbuf", [128, (N - 1) * CAP], "float32"),
-    "rr": ("sbuf", [128, n], "float32"), "ss": ("sbuf", [128, n], "float32"), "gp": ("psum", [128, n], "float32"),
+    "gp": ("psum", [128, n + BANK], "float32"), "up": ("psum", [128, 3 * BANK], "float32"),
+    "rr": ("sbuf", [128, n], "float32"), "ss": ("sbuf", [128, n], "float32"),
     "vw": ("sbuf", [128, n + (N - 1) * CAP], "float32"), "sb3": ("sbuf", [128, (N - 1) * CAP], "float32"),
-    "iw": ("sbuf", [128, 4096], "float32"), "iv": ("sbuf", [128, 4096 + SP], "float32"), "jj": ("sbuf", [128, n + (N - 1) * CAP], "float32"),
-    "fz": ("sbuf", [128, CAP], "float32"), "it": ("sbuf", [128, 256], "float32"), "iu": ("sbuf", [128, 256], "float32"),
+    "iw": ("sbuf", [128, 4096 + SP], "float32"), "iv": ("sbuf", [128, 4096 + 2 * SP], "float32"),
+    "jj": ("sbuf", [128, n + (N - 1) * CAP], "float32"),
+    "it": ("sbuf", [128, 256], "float32"), "iu": ("sbuf", [128, 256], "float32"), "ik": ("sbuf", [128, 256], "float32"),
     "uu": ("sbuf", [128, n], "float32"), "a0": ("sbuf", [128, n], "float32"), "y0": ("sbuf", [128, n], "float32"),
-    "fx": ("sbuf", [128, 16], "float32"), "tm": ("sbuf", [128, 16], "float32"), "dc": ("sbuf", [128, 4], "float32"),
-    "dq": ("sbuf", [128, 4 * N], "float32"), "on": ("sbuf", [128, 128], "float32"), "ey": ("sbuf", [128, 128], "float32"),
+    "dc": ("sbuf", [128, 4], "float32"),
+    "rb": ("sbuf", [128, HALF + 4 * N], "float32"),
+    "zf": ("sbuf", [128, 128], "float32"), "ef": ("sbuf", [128, 128], "float32"), "nf": ("sbuf", [128, 128], "float32"),
 }
 SEMAPHORES = ["a1", "a20", "a21", "a22", "a3", "a4", "sent"] + ["e%d" % k for k in range(140)]
 
@@ -53,16 +60,20 @@ def rank_program(g, core, T, topo):
         return
     cores = list(T.cores)
     turn = [(r + 1 + k) % N for k in range(N - 1)]
-    frm = [(r - 1 - k) % N for k in range(N - 1)]
     V, A, S, P = g.vector, g.scalar, g.sync, g.tensor
     sems, waited, seen, sent = {}, set(), set(), [0]
     D = T.dc[:, 0:1]
-    h = n // 2
 
     def engines(p, q):
         return len(topo.engines(cores[p], cores[q]))
-    count = {a: sum(engines(q, r) for q in frm) for a in ("a1", "a3", "a4")}
-    count.update({"a2%d" % k: engines(q, r) for k, q in enumerate(frm)})
+    def parts(w):
+        e, m = engines(r, turn[0]), len(w) // 2
+        cut = {1: [0, e], 2: [0, e // 2, e], 3: [0, e // 2, 3 * e // 4, e]}[m]
+        return [(w[2 * i], int(w[2 * i + 1]), slice(cut[i], cut[i + 1])) for i in range(m)]
+    count = {"a1": 0, "a3": 0, "a4": sum(engines(q, r) for q in turn)}
+    for a, k, part in [x for w in POOL.split() if w[0] in "XHV" for x in parts(w)]:
+        name = {"X": "a1", "H": "a2%d" % (N - 2 - k), "V": "a3"}[a]
+        count[name] = count.get(name, 0) + part.stop - part.start
 
     def sem(name):
         if name in count:
@@ -79,125 +90,136 @@ def rank_program(g, core, T, topo):
                 waited.add(e)
                 {"v": V, "a": A, "s": S, "g": g, "p": P}[qn].wait_ge(*sem(e))
 
-    def slot(t, k, base=0):
-        return t[:, base + k * CAP:base + (k + 1) * CAP]
+    def slot(t, j, base=0, k=None):
+        return t[:, base + j * CAP:base + ((j if k is None else k) + 1) * CAP]
 
-    def cols(t, q, base=0):
-        return t[:, base + q * LC:base + (q + 1) * LC]
+    def cols(t, j, base=0, k=None):
+        return t[:, base + j * LC:base + ((j if k is None else k) + 1) * LC]
+
+    def holds(a, k):
+        return [w for w in (VEC + " " + ACT + " " + POOL).split() if w.rstrip("012") == a and w[len(a)] <= str(k) <= w[-1]][0]
 
     def back(lo, hi):
         return slice(hi - 1, lo - 1 if lo else None, -1)
 
-    def pieces(name, cuts):
-        return [name + str(k) for k in range(len(cuts) - 1)]
+    def pieces(name, cuts, lo=0, hi=n):
+        return [name + str(k) for k in range(len(cuts) - 1) if min(cuts[k], cuts[k + 1]) < hi and max(cuts[k], cuts[k + 1]) > lo]
 
     def const(ap, v):
-        return g.iota(ap, [[0, ap.shape[1]]], v, 0, allow_small_or_imprecise_dtypes=True)
-
-    def count_up(lo, hi):
-        return g.iota(T.jj[:, lo:hi], [[1, hi - lo]], JB + lo, 0, allow_small_or_imprecise_dtypes=True)
+        return g.iota(ap, [[0, ap.shape[1]]], int(v), 0, allow_small_or_imprecise_dtypes=True)
 
     head0, head1, head2 = T.hu[:, 0:1], T.hu[:, 2:3], T.hu[:, 4:5]
-    d1 = T.d1[:, 16:16 + n]
-    mine = T.dq[:, 4 * r:4 * r + 1]
-    order = {a: [w for w in (VEC + " " + ACT).split() if w[:2] == a] for a in ("js", "jp")}
-    on_pe = PEQ.split()
+    every = (VEC + " " + ACT).split()
+    fz = slot(T.cw, r, n)
+    early = [w for w in VEC.split() if w[:2] == "jp"]
+    order = {"iw": [w for w in ACT.split() if w[:2] == "jp"], "iv": early + [w for w in every if w[:2] == "js"]}
+    hs = [w for w in VEC.split() if w[0] == "h" and w != "hu"]
+    s1, s2 = [["l_s%d%s" % (t, x) for x in "ab"[r == N - 1:1 + (r > 0)]] for t in (1, 2)]
+    on_pe = [k for k in range(len(Y1) - 1) if "u%d" % k not in every]
 
-    def gather(q, dst, win, bias=0.0):
-        if q == "a":
-            return A.activation(dst, win, Fn.Identity, bias=bias)
-        return V.tensor_scalar(dst, win, bias, None, Op.add)
+    def gather(q, dst, win):
+        return A.activation(dst, win, Fn.Identity) if q == "a" else V.tensor_copy(dst, win)
 
-    def from_d(q, dst, src):
+    def flip(q, dst, src, b):
         if q == "a":
-            return A.activation(dst, src, Fn.Identity, bias=D, scale=-1.0)
-        return V.tensor_scalar(dst, src, -1.0, D, Op.mult, Op.add)
+            return A.activation(dst, src, Fn.Identity, bias=b, scale=-1.0)
+        return V.tensor_scalar(dst, src, -1.0, b, Op.mult, Op.add)
+
+    def before(names, w, a):
+        names = names.split()
+        return [x for x in names[:names.index(w)] if x.rstrip("012") == a] if WAW else []
+
+    def bank(k):
+        at = on_pe.index(k) * BANK
+        return T.up[:, at:at + Y1[k + 1] - Y1[k]]
+
+    def gp(lo, hi):
+        assert hi <= GS or lo >= GS
+        return T.gp[:, lo + BANK * (lo >= GS):hi + BANK * (lo >= GS)]
+    banks, edge = range(0, n + 1, BANK), T.gp[:, GS + BANK - 1:GS + BANK]
 
     def call(q, w):
         k = int(w[-1]) if w[-1].isdigit() else 0
-        a = w.rstrip("0123456789") if w not in ("m0", "m2", "xm0", "xm2", "c0", "g1", "z0", "d1") else w
-        if w.startswith("g2"):
-            a = "g2"
+        j = int(w.lstrip("abcdefghijklmnopqrstuvwxyz")[:1] or 0)
+        a = "g2" if w[:2] == "g2" else w if w in ("m2", "xm0", "xm2", "c0", "z0", "g1") else w.rstrip("0123456789")
 
         def after(*names):
             wait(q, *names)
         if a == "fz":
-            return V.memset(T.fz[:], float(JB))
+            return V.memset(fz, float(JB))
         if a == "m2":
             return V.memset(T.m2[:], BIG)
-        if a == "m0":
-            return V.memset(T.m0[:, 0:MS], 1.0) if q == "v" else const(T.m0[:, MS:], 1)
         if a == "z0":
-            if q == "g":
-                return const(T.z0[:], 0)
-            after("gz0", "kp", "hu")
-            return V.tensor_copy(T.z0[:, 0:n].indirect(head0), T.kp[:])
-        if a == "kz":
-            return g.iota(T.kz[:], [[JB, 2], [0, 16]], 0, 0, allow_small_or_imprecise_dtypes=True)
-        if a == "kn":
-            return const(T.kn[:], -int(BIG))
-        if a == "kp":
-            return const(T.kp[:], int(BIG))
-        if a == "d1":
-            return const(T.d1[:, 0:16], 0)
+            return V.memset(T.z0[:, 0:ZV], 0.0)
+        if a == "zg":
+            return const(T.z0[:, ZV:], 0)
+        if a in ("kn", "kp", "zf", "zb"):
+            return const(T[a][:], {"kn": -BIG, "kp": RND}.get(a, 0))
+        if a in ("ef", "nf", "eb"):
+            after("z" + a[1])
+            return g.affine_select(T[a][:], T["z" + a[1]][:], [[-1, 128]], Op.not_equal, 1.0 if a[0] == "e" else -1.0, 0, 1)
         if a == "tr":
-            return g.iota(T.tr[:], [[16, SL]], 4096, 1)
-        if a == "tq":
-            return g.iota(T.tq[:], [[16, SL]], 1, 1)
-        if a == "jj":
-            return count_up(JC[k], JC[k + 1])
-        if a == "jq":
-            return count_up(n, n + (N - 1) * CAP)
-        if a == "ey":
-            done("ones", const(T.on[:], 1))
-            after("ones")
-            return g.affine_select(T.ey[:], T.on[:], [[-1, 128]], Op.is_equal, 0.0, 0, 1)
+            return g.iota(T.tr[:], [[-4095, 2], [16, SL]], 4096, 1)
+        if a in ("jj", "jq"):
+            lo, hi = (JJ[k], JJ[k + 1]) if a == "jj" else (n + j * CAP, n + (k + 1) * CAP)
+            return g.iota(T.jj[:, lo:hi], [[1, hi - lo]], JB + lo, 0, allow_small_or_imprecise_dtypes=True)
         if a == "w":
+            if q == "g":
+                return const(slot(T.w2, turn[k], SP + n), JB)
             after("fz")
-            return A.activation(slot(T.w2, turn[k], SP + n), T.fz[:], Fn.Silu)
-        if a == "cw":
-            after("fz")
-            return A.activation(slot(T.cw, r, n), T.fz[:], Fn.Identity)
+            return A.activation(slot(T.w2, turn[k], SP + n), fz, Fn.Silu)
         if a == "hu":
             after("l_hd")
             return V.tensor_copy(T.hu[:, 0:6:2], T.hd[:])
         if a == "xm2":
-            after("hu", "m2", "kz")
-            return V.tensor_copy(T.m2[:, 0:n].indirect(head2), T.kz[:, 16:32])
+            after("hu", "m2", "fz")
+            return V.tensor_copy(T.m2[:, 0:n].indirect(head2), T.cw[:, n + r * CAP:n + r * CAP + 16])
         if a == "xm0":
-            after("hu", "m0", "gm0", "kz")
-            return V.tensor_copy(T.m0[:, 0:n].indirect(head0), T.kz[:, 0:16])
+            after("hu", "z0", "kp", "zg")
+            return V.tensor_copy(T.z0[:, 0:n].indirect(head0), T.kp[:])
         if a == "op":
-            after("l_pv")
-            return V.tensor_copy(T.oa[:, SL + 128:], T.la[:, SL + 128:])
+            after("l_p2")
+            return V.tensor_copy(T.op[:], T.la[:, 0:128])
         if a == "oa":
-            after("l_pv", "l_s1")
-            return V.tensor_copy(T.oa[:, 0:SL + 128], T.la[:, 0:SL + 128])
+            after("l_p1", *s1)
+            return V.tensor_copy(T.oa[:], T.la[:, 128:256 + SL])
         if a == "t":
-            after(*([["l_pv", "l_s1"], ["t1"], ["t2", "tr"], ["t3"]][k - 1]))
+            after(*([["l_p1"] + s1, ["t1"], ["t2", "tr"], ["t3", "e2"]][k - 1]))
             if k == 1:
-                return V.tensor_scalar(T.pa[:], T.la[:, 0:SL + 128], 4097, None, Op.mult)
+                return V.tensor_scalar(T.pa[:, 0:128 + SL], T.la[:, 128:256 + SL], 4097, None, Op.mult)
             if k == 2:
-                return V.tensor_scalar(T.pa[:], T.pa[:], 4, 0x100FFF, Op.arith_shift_right, Op.bitwise_and)
+                return V.tensor_scalar(T.pa[:, 0:128 + SL], T.pa[:, 0:128 + SL], 4, 0x100FFF, Op.arith_shift_right, Op.bitwise_and)
             if k == 3:
-                return V.tensor_tensor(T.pa[:, 0:SL], T.pa[:, 0:SL], T.tr[:], Op.min)
-            return V.tensor_copy(T.ob[:], T.pa[:])
+                return V.tensor_tensor(T.pa[:, 128:128 + SL], T.pa[:, 128:128 + SL], T.tr[:, 0:SL], Op.min)
+            return V.tensor_scalar(T.ob[:], T.pa[:], SP, None, Op.add)
         if a == "e":
-            after(*([["l_s2", "tq"], ["e1"], ["e2"]][k - 1]))
+            after(*([s2 + ["tr"], ["e1"]][k - 1]))
             if k == 1:
-                return V.tensor_tensor(T.pc[:], T.lb[:], T.tq[:], Op.mult)
-            if k == 2:
-                return V.tensor_tensor(T.pc[:], T.pc[:], T.lb[:], Op.min)
-            return V.tensor_scalar(T.oc[:], T.pc[:], SP, None, Op.add)
+                return V.tensor_tensor(T.pa[:, 128 + SL:], T.la[:, 256 + SL:], T.tr[:, SL:], Op.mult)
+            return V.tensor_tensor(T.pa[:, 128 + SL:], T.pa[:, 128 + SL:], T.la[:, 256 + SL:], Op.min)
         if a in ("js", "jp"):
-            at = order[a].index(w)
-            after("t4", order[a][at - 1] if at else "l_iw" if a == "jp" else "l_iv", "jq" if a == "js" else "jj%d" % k)
+            name = "iw" if w in order["iw"] else "iv"
+            mine = (VEC if q == "v" else ACT).split()
+            after("t4", "l_" + name, *(["l_ik"] if a == "js" and early else []))
+            after(*[x for x in order[name][:order[name].index(w)] if WAW or x not in mine])
             if a == "js":
-                win, src = T.iv[:].indirect(cols(T.ob, frm[k])), slot(T.jj, k, n)
+                win, lo, hi = T.iv[:].indirect(cols(T.ob, j, 128, k)), n + j * CAP, n + (k + 1) * CAP
             else:
-                win, src = T.iw[:].indirect(T.ob[:, SL + JC[k] // 16:SL + JC[k + 1] // 16]), T.jj[:, JC[k]:JC[k + 1]]
-            return V.tensor_copy(win, src) if q == "v" else A.activation(win, src, Fn.Silu)
+                win, lo, hi = T[name][:].indirect(T.ob[:, JC[k] // 16:JC[k + 1] // 16]), JC[k], JC[k + 1]
+            if q == "v":
+                assert hi - lo <= JJ[-1]
+                after(*pieces("jj", JJ, 0, hi - lo))
+                return V.tensor_scalar(win, T.jj[:, 0:hi - lo], 1.0, float(lo), Op.mult, Op.add)
+            assert a == "js" or hi <= JJ[-1]
+            after(*([holds("jq", x) for x in range(j, k + 1)] if a == "js" else pieces("jj", JJ, lo, hi)))
+            return A.activation(win, T.jj[:, lo:hi], Fn.Silu)
+        if a == "ok":
+            after("l_it", "l_ik")
+            return V.tensor_tensor(T.ik[:, 128:208], T.ik[:, 128:208], T.it[:, 128:208], Op.add)
         if a == "oi":
+            if early:
+                after("ok")
+                return V.tensor_scalar(T.oi[:, 128:], T.ik[:, 128:208], 0.25 - 2 * JB, None, Op.add)
             after("l_it")
             return V.tensor_scalar(T.oi[:, 128:], T.it[:, 128:208], 0.25 - JB, None, Op.add)
         if a == "om":
@@ -208,79 +230,82 @@ def rank_program(g, core, T, topo):
             return V.tensor_scalar(T.oi[:, 0:128], T.iu[:, 0:128], 0.25 - 2 * JB, None, Op.add)
         if a == "c0":
             after("l_d0", "xm0")
-            return V.tensor_tensor_scan(T.cw[:, 0:n], T.m0[:, 0:n], T.d0[:], 0.0, Op.mult, Op.add)
+            return V.tensor_tensor_scan(T.cw[:, 0:n], T.z0[:, 0:n], T.d0[:], 0.0, Op.max, Op.subtract)
         if a == "x":
             after("oa", "c0")
-            return gather(q, slot(T.sb1, k), T.cw[:, 0:n].indirect(cols(T.oa, turn[k])))
+            return gather(q, slot(T.sb1, j, 0, k), T.cw[:, 0:n].indirect(cols(T.oa, j, 128, k)))
         if a == "r":
-            after("a1", "cw", "oa", "c0")
-            return gather(q, T.rr[:, RC[k]:RC[k + 1]], T.cw[:].indirect(T.oa[:, SL + RC[k] // 16:SL + RC[k + 1] // 16]), RND)
+            after("a1", "fz", "oa", "c0")
+            return flip(q, T.rr[:, RC[k]:RC[k + 1]], T.cw[:].indirect(T.oa[:, RC[k] // 16:RC[k + 1] // 16]), 2 * RND)
         if a == "g2":
             hi, lo = C2[k], C2[k + 1]
-            after("xm2", *["l_d2%d" % j for j in range(len(L2) - 1) if L2[j] > lo])
+            after("xm2", *pieces("l_d2", L2, lo, hi))
             if k:
                 after("g2%d" % (k - 1))
             return V.tensor_tensor_scan(T.g2[:, back(lo, hi)], T.m2[:, hi:lo:-1], T.d2[:, back(lo, hi)],
                                         T.g2[:, hi:hi + 1] if k else float(JB), Op.min, Op.add)
         if a == "p":
             hi, lo = C2[k], C2[k + 1]
-            after("op", "g2%d" % k, *(["p%d" % (k - 1)] if k else pieces("w", range(N))))
-            return A.activation(T.w2[:, SP:].indirect(T.oa[:, SL + 128 + lo // 16:SL + 128 + hi // 16]), T.g2[:, lo:hi], Fn.Silu)
+            after("op", "g2%d" % k, "w0", "w1", "w2", *before(ACT, w, "p"))
+            return A.activation(T.w2[:, SP:].indirect(T.op[:, lo // 16:hi // 16]), T.g2[:, lo:hi], Fn.Silu)
         if a == "h":
-            after("a2%d" % k, "e3", "h%d" % (k - 1) if k else pieces("p", C2)[-1])
-            return V.tensor_copy(T.w2[:, 0:SP + n].indirect(cols(T.oc, frm[k])), slot(T.r2, k))
-        if a == "fx":
-            after("l_d1", "hu")
-            return V.tensor_scalar(T.fx[:], d1.indirect(head1), BIG, None, Op.add)
-        if a == "xd":
-            after("fx", "kn")
-            return V.tensor_copy(d1.indirect(head1), T.kn[:])
+            after("t4", *pieces("p", C2), *before(VEC, w, "h"), *["a2%d" % x for x in range(j, k + 1)])
+            return V.tensor_copy(T.w2[:, 0:SP + n].indirect(cols(T.ob, j, 128 + SL, k)), slot(T.r2, j, 0, k))
+        if a in ("xa", "xb"):
+            after("l_d" + a[1], "hu", "kn")
+            return V.tensor_copy(T["d" + a[1]][:, 0:n].indirect(head1), T.kn[:])
         if a == "o":
-            after("xm0")
-            return P.matmul(T.gp[:, k * BANK:(k + 1) * BANK], T.m0[:, 0:128], T.m0[:, 0:BANK], True, False)
-        if a == "g1":
-            after("h%d" % (N - 2), "xd", *[x for x in on_pe if x[0] == "o"])
-            return V.tensor_tensor_scan(T.gp[:, ::-1], T.w2[:, SP + n - 1:SP - 1:-1], T.d1[:, n + 15:15:-1], 0.0, Op.max, Op.add)
-        if a == "tm":
-            after("fx", *pieces("r", RC))
-            return V.tensor_tensor(T.tm[:], T.rr[:].indirect(head1), T.fx[:], Op.add)
-        if a == "rf":
-            after("tm")
-            return V.tensor_copy(T.rr[:].indirect(head1), T.tm[:])
+            after("xm2")
+            return P.matmul(gp(k * BANK, (k + 1) * BANK), T.m2[:, 0:128], T.m2[:, 0:BANK], True, False)
+        if a == "ga":
+            after("xa", *hs, *pieces("o", banks, GS, n))
+            return V.tensor_tensor_scan(T.gp[:, back(GS + BANK - 1, n + BANK)], T.da[:, back(GS, n + 1)], T.w2[:, back(SP + GS - 1, SP + n)], -BIG, Op.add, Op.max)
+        if a == "gb":
+            after("ga", *pieces("o", banks, 0, GS))
+            return V.tensor_tensor_scan(T.gp[:, back(0, GS - 1)], T.da[:, back(1, GS)], T.w2[:, back(SP, SP + GS - 1)], edge, Op.add, Op.max)
+        if a == "gz":
+            after("ga", *pieces("o", banks, GS - 1, GS))
+            return V.tensor_copy(T.gp[:, GS - 1:GS], edge)
+        if a == "d":
+            lo, hi = k * BANK, (k + 1) * BANK
+            after("eb", "l_d1", *(["ga"] if lo >= GS else ["gb", "gz"]))
+            return P.matmul(gp(lo, hi), T.eb[:], T.d1[:, lo:hi], False, True)
         if a == "vv":
-            after("g1", "rf")
-            return V.tensor_tensor(T.vw[:, 0:n], T.gp[:], T.rr[:], Op.add)
+            lo, hi = VC[k], VC[k + 1]
+            after(*pieces("d", banks, lo, hi), *pieces("r", RC, lo, hi))
+            return V.tensor_tensor(T.vw[:, lo:hi], gp(lo, hi), T.rr[:, lo:hi], Op.add)
         if a == "red":
-            after("vv")
-            done("run", V.tensor_tensor_scan(T.y0[:, 0:h], T.vw[:, 0:h], T.vw[:, h:n], 0.0, Op.max, Op.max))
-            after("run")
-            return V.tensor_copy(mine, T.y0[:, h - 1:h])
-        if a == "v":
-            after("vv", "oi")
-            return gather(q, slot(T.sb3, k), T.vw[:, 0:n].indirect(cols(T.oi, turn[k], 128)))
-        if a == "ss":
-            lo, hi = Y1[k], Y1[k + 1]
-            after("rf", "xd", "d1", *(["ss%d" % (k - 1)] if k else []))
-            return V.tensor_tensor_scan(T.ss[:, lo:hi], T.d1[:, 15 + lo:15 + hi], T.rr[:, lo:hi], T.ss[:, lo - 1:lo] if k else 0.0, Op.add, Op.max)
+            after(*pieces("vv", VC))
+            return V.tensor_tensor_scan(T.rb[:, 0:HALF], T.vw[:, 0:HALF], T.vw[:, HALF:n], 0.0, Op.max, Op.max)
         if a == "dd":
             after("red", "a4")
-            return V.tensor_reduce(D, T.dq[:, ::4], Ax.X, Op.max)
+            return V.tensor_reduce(D, T.rb[:, HALF - 1:HALF + 4 * N - 4:4], Ax.X, Op.max)
+        if a == "ss":
+            lo, hi = Y1[k], Y1[k + 1]
+            after("xb", *pieces("r", RC, lo, hi), *(["ss%d" % (k - 1)] if k else []))
+            return V.tensor_tensor_scan(T.ss[:, lo:hi], T.db[:, lo:hi], T.rr[:, lo:hi], T.ss[:, lo - 1:lo] if k else 0.0, Op.add, Op.max)
+        if a in ("pa", "pb", "pc"):
+            lo, hi = Y1[k], Y1[k + 1]
+            assert hi - lo <= BANK
+            after(*{"pa": ["nf"] + pieces("r", RC, lo, hi), "pb": ["ef"] + pieces("vv", VC, lo, hi), "pc": ["ef", "ss%d" % k]}[a])
+            return P.matmul(bank(k), T.nf[:] if a == "pa" else T.ef[:], {"pa": T.rr, "pb": T.vw, "pc": T.ss}[a][:, lo:hi], a == "pa", a == "pc")
         if a == "u":
             lo, hi = Y1[k], Y1[k + 1]
-            after("ss%d" % k, "g1")
-            if q == "p":
-                after("vv", "ey")
-                return P.matmul(T.gp[:, lo:hi], T.ey[:], T.ss[:, lo:hi], False, True)
-            return V.tensor_tensor(T.uu[:, lo:hi], T.gp[:, lo:hi], T.ss[:, lo:hi], Op.add)
+            after("ss%d" % k, *pieces("d", banks, lo, hi))
+            return V.tensor_tensor(T.uu[:, lo:hi], gp(lo, hi), T.ss[:, lo:hi], Op.add)
         if a == "n":
-            after("u%d" % k, "dd")
-            return from_d(q, T.uu[:, Y1[k]:Y1[k + 1]], (T.gp if "u%d" % k in on_pe else T.uu)[:, Y1[k]:Y1[k + 1]])
+            lo, hi = Y1[k], Y1[k + 1]
+            after(("pc%d" if k in on_pe else "u%d") % k, "dd")
+            return flip(q, T.uu[:, lo:hi], bank(k) if k in on_pe else T.uu[:, lo:hi], D)
+        if a == "v":
+            after("oi", *pieces("vv", VC))
+            return gather(q, slot(T.sb3, k), T.vw[:, 0:n].indirect(cols(T.oi, turn[k], 128)))
         if a == "q":
             after("a3", "dd", "on")
-            return from_d(q, T.a0[:, Y0[k]:Y0[k + 1]], T.vw[:].indirect(T.oi[:, Y0[k] // 16:Y0[k + 1] // 16]))
+            return flip(q, T.a0[:, Y0[k]:Y0[k + 1]], T.vw[:].indirect(T.oi[:, Y0[k] // 16:Y0[k + 1] // 16]), D)
         if a == "b":
             lo, hi = Y0[k], Y0[k + 1]
-            after("q%d" % k, "z0", "red")
+            after("q%d" % k, "xm0")
             if hi < n:
                 after("b%d" % (k + 1))
             return V.tensor_tensor_scan(T.y0[:, back(lo, hi)], T.z0[:, hi:lo:-1], T.a0[:, back(lo, hi)],
@@ -291,33 +316,49 @@ def rank_program(g, core, T, topo):
         if w == "mx":
             wait("g", "red")
             ids = [DstId(rid=topo.addr(cores[q])[0], pnc=topo.addr(cores[q])[1]) for q in turn]
+            at = [HALF - 1 + 4 * j for j in range(N)]
             g.remote_dma_fused([RemoteDMATransfer(dst_ids=ids, dma_engine_mask=topo.mask(core, cores[turn[0]]), remote_sem=T.sem.a4,
-                                                  srcs=[mine], dsts=[mine for p in turn])], local_sem=T.sem.sent)
+                                                  srcs=[T.rb[:, at[0]:at[0] + 1]], dsts=[T.rb[:, j:j + 1] for j in at[1:]])], local_sem=T.sem.sent)
             sent[0] += engines(r, turn[0])
             return
-        k = int(w[1])
-        q = turn[k]
-        ready, dst, src, name = {"X": ("x%d" % k, slot(T.cw, r, n), slot(T.sb1, k), "a1"),
-                                 "H": (pieces("p", C2)[-1], slot(T.r2, k), slot(T.w2, q, SP + n), "a2%d" % k),
-                                 "V": ("v%d" % k, slot(T.vw, k, n), slot(T.sb3, k), "a3")}[w[0]]
-        wait("g", ready)
-        rid, pid, _ = topo.addr(cores[q])
-        g.remote_dma(dst, src, T.sem[name], T.sem.sent, pid, rid, topo.mask(core, cores[q]))
-        sent[0] += engines(r, q)
+        moves = []
+        for a, k, part in parts(w):
+            q = turn[k]
+            j = N - 2 - k
+            ready, dst, src, name = {"X": ([holds("x", k)], slot(T.cw, r, n), slot(T.sb1, k), "a1"),
+                                     "H": (pieces("p", C2), slot(T.r2, j), slot(T.w2, q, SP + n), "a2%d" % j),
+                                     "V": (["v%d" % k], slot(T.vw, j, n), slot(T.sb3, k), "a3")}[a]
+            wait("g", *ready)
+            rid, pid, _ = topo.addr(cores[q])
+            use = topo.engines(core, cores[q])[part]
+            moves.append(RemoteDMATransfer(dst_ids=[DstId(rid=rid, pnc=pid)], dma_engine_mask=sum(1 << e for e in use), remote_sem=T.sem[name], src=src, dst=dst))
+            sent[0] += len(use)
+        if len(moves) > 1:
+            g.remote_dma_fused(moves, local_sem=T.sem.sent)
+        else:
+            g.remote_dma(dst, src, T.sem[name], T.sem.sent, pid, rid, topo.mask(core, cores[q]))
 
     done("l_hd", A.dma_start(T.hd[:], T.heads[:]))
-    done("l_pv", A.dma_start(T.la[:, SL:], T.prev[:]))
     for w in LOADS.split():
         if w[0] == "i":
             wait("s", "fz")
-            x = S.dma_start(T[w][::16, 0:4096], T.fz[:, 0:256])
+            x = S.dma_start(T[w][::16, SP:SP + 4096], T.cw[:, n + r * CAP:n + r * CAP + 256])
         elif w[:2] == "d2":
             hi, lo = L2[int(w[2])], L2[int(w[2]) + 1]
             x = S.dma_start(T.d2[:, lo:hi], T.dur[:, 2 * n + lo:2 * n + hi])
         elif w[0] == "s":
-            x = S.dma_start(T.la[:, 0:SL], T.ship[:, 0:SL]) if w == "s1" else S.dma_start(T.lb[:], T.ship[:, SL:])
+            t = int(w[1]) - 1
+            lo, hi, at = (r + 1, N, 0) if w[2] == "a" else (0, r, N - 1 - r)
+            if lo == hi:
+                continue
+            x = S.dma_start(cols(T.la, at, 256 + t * SL, at + hi - lo - 1), cols(T.ship, lo, t * N * LC, hi - 1))
+        elif w == "p2":
+            x = S.dma_start(T.la[:, 0:128], T.prev[:, 128:])
+        elif w == "p1":
+            x = S.dma_start(T.la[:, 128:256], T.prev[:, 0:128])
         else:
-            x = S.dma_start(T.d0[:], T.dur[:, 0:n]) if w == "d0" else S.dma_start(d1, T.dur[:, n:2 * n])
+            lo, hi = {"d0": (0, n), "d1": (n, 2 * n), "da": (n, 2 * n + 16), "db": (n - 1, 2 * n - 1)}[w]
+            x = S.dma_start(T[w][:], T.dur[:, lo:hi])
         done("l_" + w, x)
     for q, names in (("v", VEC), ("a", ACT), ("p", PEQ)):
         for w in names.split():
@@ -326,11 +367,11 @@ def rank_program(g, core, T, topo):
         if w[0] in "XHV" or w == "mx":
             remote(w)
         else:
-            done("g" + w if w in ("m0", "z0") else w, call("g", w))
+            done(w, call("g", w))
     for w in STORES.split():
         if w[0] == "i":
-            wait("s", order["jp" if w == "it" else "js"][-1])
-            x = S.dma_start(T[w][:], (T.iw if w == "it" else T.iv)[::16, 0:4096])
+            wait("s", *{"it": order["iw"], "ik": early, "iu": order["iv"]}[w])
+            x = S.dma_start(T[w][:], (T.iw if w == "it" else T.iv)[::16, SP:SP + 4096])
         else:
             wait("s", w)
             cut, src, base = (Y1, T.uu, n) if w[0] == "n" else (Y0, T.y0, 0)

from concourse.bass import DstId, RemoteDMATransfer
from concourse.mybir import AluOpType as Op, AxisListType as Ax, ActivationFunctionType as Fn

N, n, CAP = 4, 2048, 320
BIG = float(1 << 20)
RND = float(3 << 22)
LC = CAP // 16
SL = (N - 1) * LC
SP = 1088
JB = 64
BANK = 512
HALF = n // 2
WAW = True
GS = 1024
C2 = [2048, 1696, 640, 0]
L2 = C2
JC = [0, 832, 2048]
JJ = [0, 1216]
RC = [0, 448, 2048]
VC = [0, 512, 1024, 2048]
Y0 = [0, 288, 928, 1472, 2048]
Y1 = [0, 704, 1120, 1760, 2048]
ZV = 1232
LOADS = "p2 d20 d21 d0 p1 d22 s1a s1b s2a s2b iv iw da db d1"
VEC = "fz m2 z0 hu xm2 op g20 xm0 g21 c0 oa g22 t1 e1 t2 xb e2 t3 xa t4 jp1 h2 h01 ga ok gz gb vv2 vv1 vv0 oi red ss0 ss1 u0 ss2 dd om u2 on ss3 q3 u3 b3 b2 b1 b0"
ACT = "w1 w0 p0 p1 x0 p2 x1 x2 jp0 r1 js2 r0 js01 v1 v0 v2 n0 n1 n2 q2 q1 n3 q0"
POOL = "w2 zg kp zb tr jj0 kn zf X0 H0 H1 H2 X1 X2 eb jq01 jq2 ef nf mx V1 V0 V2"
PEQ = "o3 o2 o1 o0 d3 d2 d1 d0 pa1 pb1 pc1"
STORES = "ik it iu n0 n1 n2 b3 b2 n3 b1 b0"

SCRATCH = {
    "d0": ("sbuf", [128, n], "bfloat16"), "d2": ("sbuf", [128, n], "bfloat16"), "d1": ("sbuf", [128, n], "bfloat16"),
    "da": ("sbuf", [128, n + 16], "bfloat16"), "db": ("sbuf", [128, n], "bfloat16"),
    "zb": ("sbuf", [128, 128], "bfloat16"), "eb": ("sbuf", [128, 128], "bfloat16"),
    "m2": ("sbuf", [128, n + 16], "bfloat16"), "z0": ("sbuf", [128, n + 16], "bfloat16"),
    "kn": ("sbuf", [128, 16], "bfloat16"), "kp": ("sbuf", [128, 16], "bfloat16"),
    "hd": ("sbuf", [128, 3], "int32"), "hu": ("sbuf", [128, 6], "uint16"),
    "la": ("sbuf", [128, 256 + 2 * SL], "int32"), "tr": ("sbuf", [128, 2 * SL], "int32"), "pa": ("sbuf", [128, 128 + 2 * SL], "int32"),
    "op": ("sbuf", [128, 128], "uint16"), "oa": ("sbuf", [128, 128 + SL], "uint16"), "ob": ("sbuf", [128, 128 + 2 * SL], "uint16"),
    "oi": ("sbuf", [128, 208], "uint16"),
    "cw": ("sbuf", [128, n + N * CAP], "float32"), "sb1": ("sbuf", [128, (N - 1) * CAP], "float32"),
    "g2": ("sbuf", [128, n], "float32"), "w2": ("sbuf", [128, SP + n + N * CAP], "float32"), "r2": ("sbuf", [128, (N - 1) * CAP], "float32"),
    "gp": ("psum", [128, n + BANK], "float32"), "up": ("psum", [128, 3 * BANK], "float32"),
    "rr": ("sbuf", [128, n], "float32"), "ss": ("sbuf", [128, n], "float32"),
    "vw": ("sbuf", [128, n + (N - 1) * CAP], "float32"), "sb3": ("sbuf", [128, (N - 1) * CAP], "float32"),
    "iw": ("sbuf", [128, 4096 + SP], "float32"), "iv": ("sbuf", [128, 4096 + 2 * SP], "float32"),
    "jj": ("sbuf", [128, n + (N - 1) * CAP], "float32"),
    "it": ("sbuf", [128, 256], "float32"), "iu": ("sbuf", [128, 256], "float32"), "ik": ("sbuf", [128, 256], "float32"),
    "uu": ("sbuf", [128, n], "float32"), "a0": ("sbuf", [128, n], "float32"), "y0": ("sbuf", [128, n], "float32"),
    "dc": ("sbuf", [128, 4], "float32"),
    "rb": ("sbuf", [128, HALF + 4 * N], "float32"),
    "zf": ("sbuf", [128, 128], "float32"), "ef": ("sbuf", [128, 128], "float32"), "nf": ("sbuf", [128, 128], "float32"),
}
SEMAPHORES = ["a1", "a20", "a21", "a22", "a3", "a4", "sent"] + ["e%d" % k for k in range(140)]


def rank_program(g, core, T, topo):
    r = T.rank_of(core)
    if r is None:
        return
    cores = list(T.cores)
    turn = [(r + 1 + k) % N for k in range(N - 1)]
    V, A, S, P = g.vector, g.scalar, g.sync, g.tensor
    sems, waited, seen, sent = {}, set(), set(), [0]
    D = T.dc[:, 0:1]

    def engines(p, q):
        return len(topo.engines(cores[p], cores[q]))
    def parts(w):
        e, m = engines(r, turn[0]), len(w) // 2
        cut = {1: [0, e], 2: [0, e // 2, e], 3: [0, e // 2, 3 * e // 4, e]}[m]
        return [(w[2 * i], int(w[2 * i + 1]), slice(cut[i], cut[i + 1])) for i in range(m)]
    count = {"a1": 0, "a3": 0, "a4": sum(engines(q, r) for q in turn)}
    for a, k, part in [x for w in POOL.split() if w[0] in "XHV" for x in parts(w)]:
        name = {"X": "a1", "H": "a2%d" % (N - 2 - k), "V": "a3"}[a]
        count[name] = count.get(name, 0) + part.stop - part.start

    def sem(name):
        if name in count:
            return T.sem[name], count[name]
        return T.sem[sems.setdefault(name, "e%d" % len(sems))], 16 if name.startswith("l_") else 1

    def done(name, ins):
        ins.then_inc(*sem(name))

    def wait(qn, *names):
        for e in names:
            if (qn, e) not in seen:
                seen.add((qn, e))
                waited.add(e)
                {"v": V, "a": A, "s": S, "g": g, "p": P}[qn].wait_ge(*sem(e))

    def slot(t, j, base=0, k=None):
        return t[:, base + j * CAP:base + ((j if k is None else k) + 1) * CAP]

    def cols(t, j, base=0, k=None):
        return t[:, base + j * LC:base + ((j if k is None else k) + 1) * LC]

    def holds(a, k):
        return [w for w in (VEC + " " + ACT + " " + POOL).split() if w.rstrip("012") == a and w[len(a)] <= str(k) <= w[-1]][0]

    def back(lo, hi):
        return slice(hi - 1, lo - 1 if lo else None, -1)

    def pieces(name, cuts, lo=0, hi=n):
        return [name + str(k) for k in range(len(cuts) - 1) if min(cuts[k], cuts[k + 1]) < hi and max(cuts[k], cuts[k + 1]) > lo]

    def const(ap, v):
        return g.iota(ap, [[0, ap.shape[1]]], int(v), 0, allow_small_or_imprecise_dtypes=True)

    head0, head1, head2 = T.hu[:, 0:1], T.hu[:, 2:3], T.hu[:, 4:5]
    every = (VEC + " " + ACT).split()
    fz = slot(T.cw, r, n)
    early = [w for w in VEC.split() if w[:2] == "jp"]
    order = {"iw": [w for w in ACT.split() if w[:2] == "jp"], "iv": early + [w for w in every if w[:2] == "js"]}
    hs = [w for w in VEC.split() if w[0] == "h" and w != "hu"]
    s1, s2 = [["l_s%d%s" % (t, x) for x in "ab"[r == N - 1:1 + (r > 0)]] for t in (1, 2)]
    on_pe = [k for k in range(len(Y1) - 1) if "u%d" % k not in every]

    def gather(q, dst, win):
        return A.activation(dst, win, Fn.Identity) if q == "a" else V.tensor_copy(dst, win)

    def flip(q, dst, src, b):
        if q == "a":
            return A.activation(dst, src, Fn.Identity, bias=b, scale=-1.0)
        return V.tensor_scalar(dst, src, -1.0, b, Op.mult, Op.add)

    def before(names, w, a):
        names = names.split()
        return [x for x in names[:names.index(w)] if x.rstrip("012") == a] if WAW else []

    def bank(k):
        at = on_pe.index(k) * BANK
        return T.up[:, at:at + Y1[k + 1] - Y1[k]]

    def gp(lo, hi):
        assert hi <= GS or lo >= GS
        return T.gp[:, lo + BANK * (lo >= GS):hi + BANK * (lo >= GS)]
    banks, edge = range(0, n + 1, BANK), T.gp[:, GS + BANK - 1:GS + BANK]

    def call(q, w):
        k = int(w[-1]) if w[-1].isdigit() else 0
        j = int(w.lstrip("abcdefghijklmnopqrstuvwxyz")[:1] or 0)
        a = "g2" if w[:2] == "g2" else w if w in ("m2", "xm0", "xm2", "c0", "z0", "g1") else w.rstrip("0123456789")

        def after(*names):
            wait(q, *names)
        if a == "fz":
            return V.memset(fz, float(JB))
        if a == "m2":
            return V.memset(T.m2[:], BIG)
        if a == "z0":
            return V.memset(T.z0[:, 0:ZV], 0.0)
        if a == "zg":
            return const(T.z0[:, ZV:], 0)
        if a in ("kn", "kp", "zf", "zb"):
            return const(T[a][:], {"kn": -BIG, "kp": RND}.get(a, 0))
        if a in ("ef", "nf", "eb"):
            after("z" + a[1])
            return g.affine_select(T[a][:], T["z" + a[1]][:], [[-1, 128]], Op.not_equal, 1.0 if a[0] == "e" else -1.0, 0, 1)
        if a == "tr":
            return g.iota(T.tr[:], [[-4095, 2], [16, SL]], 4096, 1)
        if a in ("jj", "jq"):
            lo, hi = (JJ[k], JJ[k + 1]) if a == "jj" else (n + j * CAP, n + (k + 1) * CAP)
            return g.iota(T.jj[:, lo:hi], [[1, hi - lo]], JB + lo, 0, allow_small_or_imprecise_dtypes=True)
        if a == "w":
            if q == "g":
                return const(slot(T.w2, turn[k], SP + n), JB)
            after("fz")
            return A.activation(slot(T.w2, turn[k], SP + n), fz, Fn.Silu)
        if a == "hu":
            after("l_hd")
            return V.tensor_copy(T.hu[:, 0:6:2], T.hd[:])
        if a == "xm2":
            after("hu", "m2", "fz")
            return V.tensor_copy(T.m2[:, 0:n].indirect(head2), T.cw[:, n + r * CAP:n + r * CAP + 16])
        if a == "xm0":
            after("hu", "z0", "kp", "zg")
            return V.tensor_copy(T.z0[:, 0:n].indirect(head0), T.kp[:])
        if a == "op":
            after("l_p2")
            return V.tensor_copy(T.op[:], T.la[:, 0:128])
        if a == "oa":
            after("l_p1", *s1)
            return V.tensor_copy(T.oa[:], T.la[:, 128:256 + SL])
        if a == "t":
            after(*([["l_p1"] + s1, ["t1"], ["t2", "tr"], ["t3", "e2"]][k - 1]))
            if k == 1:
                return V.tensor_scalar(T.pa[:, 0:128 + SL], T.la[:, 128:256 + SL], 4097, None, Op.mult)
            if k == 2:
                return V.tensor_scalar(T.pa[:, 0:128 + SL], T.pa[:, 0:128 + SL], 4, 0x100FFF, Op.arith_shift_right, Op.bitwise_and)
            if k == 3:
                return V.tensor_tensor(T.pa[:, 128:128 + SL], T.pa[:, 128:128 + SL], T.tr[:, 0:SL], Op.min)
            return V.tensor_scalar(T.ob[:], T.pa[:], SP, None, Op.add)
        if a == "e":
            after(*([s2 + ["tr"], ["e1"]][k - 1]))
            if k == 1:
                return V.tensor_tensor(T.pa[:, 128 + SL:], T.la[:, 256 + SL:], T.tr[:, SL:], Op.mult)
            return V.tensor_tensor(T.pa[:, 128 + SL:], T.pa[:, 128 + SL:], T.la[:, 256 + SL:], Op.min)
        if a in ("js", "jp"):
            name = "iw" if w in order["iw"] else "iv"
            mine = (VEC if q == "v" else ACT).split()
            after("t4", "l_" + name, *(["l_ik"] if a == "js" and early else []))
            after(*[x for x in order[name][:order[name].index(w)] if WAW or x not in mine])
            if a == "js":
                win, lo, hi = T.iv[:].indirect(cols(T.ob, j, 128, k)), n + j * CAP, n + (k + 1) * CAP
            else:
                win, lo, hi = T[name][:].indirect(T.ob[:, JC[k] // 16:JC[k + 1] // 16]), JC[k], JC[k + 1]
            if q == "v":
                assert hi - lo <= JJ[-1]
                after(*pieces("jj", JJ, 0, hi - lo))
                return V.tensor_scalar(win, T.jj[:, 0:hi - lo], 1.0, float(lo), Op.mult, Op.add)
            assert a == "js" or hi <= JJ[-1]
            after(*([holds("jq", x) for x in range(j, k + 1)] if a == "js" else pieces("jj", JJ, lo, hi)))
            return A.activation(win, T.jj[:, lo:hi], Fn.Silu)
        if a == "ok":
            after("l_it", "l_ik")
            return V.tensor_tensor(T.ik[:, 128:208], T.ik[:, 128:208], T.it[:, 128:208], Op.add)
        if a == "oi":
            if early:
                after("ok")
                return V.tensor_scalar(T.oi[:, 128:], T.ik[:, 128:208], 0.25 - 2 * JB, None, Op.add)
            after("l_it")
            return V.tensor_scalar(T.oi[:, 128:], T.it[:, 128:208], 0.25 - JB, None, Op.add)
        if a == "om":
            after("l_it", "l_iu")
            return V.tensor_tensor(T.iu[:, 0:128], T.iu[:, 0:128], T.it[:, 0:128], Op.add)
        if a == "on":
            after("om")
            return V.tensor_scalar(T.oi[:, 0:128], T.iu[:, 0:128], 0.25 - 2 * JB, None, Op.add)
        if a == "c0":
            after("l_d0", "xm0")
            return V.tensor_tensor_scan(T.cw[:, 0:n], T.z0[:, 0:n], T.d0[:], 0.0, Op.max, Op.subtract)
        if a == "x":
            after("oa", "c0")
            return gather(q, slot(T.sb1, j, 0, k), T.cw[:, 0:n].indirect(cols(T.oa, j, 128, k)))
        if a == "r":
            after("a1", "fz", "oa", "c0")
            return flip(q, T.rr[:, RC[k]:RC[k + 1]], T.cw[:].indirect(T.oa[:, RC[k] // 16:RC[k + 1] // 16]), 2 * RND)
        if a == "g2":
            hi, lo = C2[k], C2[k + 1]
            after("xm2", *pieces("l_d2", L2, lo, hi))
            if k:
                after("g2%d" % (k - 1))
            return V.tensor_tensor_scan(T.g2[:, back(lo, hi)], T.m2[:, hi:lo:-1], T.d2[:, back(lo, hi)],
                                        T.g2[:, hi:hi + 1] if k else float(JB), Op.min, Op.add)
        if a == "p":
            hi, lo = C2[k], C2[k + 1]
            after("op", "g2%d" % k, "w0", "w1", "w2", *before(ACT, w, "p"))
            return A.activation(T.w2[:, SP:].indirect(T.op[:, lo // 16:hi // 16]), T.g2[:, lo:hi], Fn.Silu)
        if a == "h":
            after("t4", *pieces("p", C2), *before(VEC, w, "h"), *["a2%d" % x for x in range(j, k + 1)])
            return V.tensor_copy(T.w2[:, 0:SP + n].indirect(cols(T.ob, j, 128 + SL, k)), slot(T.r2, j, 0, k))
        if a in ("xa", "xb"):
            after("l_d" + a[1], "hu", "kn")
            return V.tensor_copy(T["d" + a[1]][:, 0:n].indirect(head1), T.kn[:])
        if a == "o":
            after("xm2")
            return P.matmul(gp(k * BANK, (k + 1) * BANK), T.m2[:, 0:128], T.m2[:, 0:BANK], True, False)
        if a == "ga":
            after("xa", *hs, *pieces("o", banks, GS, n))
            return V.tensor_tensor_scan(T.gp[:, back(GS + BANK - 1, n + BANK)], T.da[:, back(GS, n + 1)], T.w2[:, back(SP + GS - 1, SP + n)], -BIG, Op.add, Op.max)
        if a == "gb":
            after("ga", *pieces("o", banks, 0, GS))
            return V.tensor_tensor_scan(T.gp[:, back(0, GS - 1)], T.da[:, back(1, GS)], T.w2[:, back(SP, SP + GS - 1)], edge, Op.add, Op.max)
        if a == "gz":
            after("ga", *pieces("o", banks, GS - 1, GS))
            return V.tensor_copy(T.gp[:, GS - 1:GS], edge)
        if a == "d":
            lo, hi = k * BANK, (k + 1) * BANK
            after("eb", "l_d1", *(["ga"] if lo >= GS else ["gb", "gz"]))
            return P.matmul(gp(lo, hi), T.eb[:], T.d1[:, lo:hi], False, True)
        if a == "vv":
            lo, hi = VC[k], VC[k + 1]
            after(*pieces("d", banks, lo, hi), *pieces("r", RC, lo, hi))
            return V.tensor_tensor(T.vw[:, lo:hi], gp(lo, hi), T.rr[:, lo:hi], Op.add)
        if a == "red":
            after(*pieces("vv", VC))
            return V.tensor_tensor_scan(T.rb[:, 0:HALF], T.vw[:, 0:HALF], T.vw[:, HALF:n], 0.0, Op.max, Op.max)
        if a == "dd":
            after("red", "a4")
            return V.tensor_reduce(D, T.rb[:, HALF - 1:HALF + 4 * N - 4:4], Ax.X, Op.max)
        if a == "ss":
            lo, hi = Y1[k], Y1[k + 1]
            after("xb", *pieces("r", RC, lo, hi), *(["ss%d" % (k - 1)] if k else []))
            return V.tensor_tensor_scan(T.ss[:, lo:hi], T.db[:, lo:hi], T.rr[:, lo:hi], T.ss[:, lo - 1:lo] if k else 0.0, Op.add, Op.max)
        if a in ("pa", "pb", "pc"):
            lo, hi = Y1[k], Y1[k + 1]
            assert hi - lo <= BANK
            after(*{"pa": ["nf"] + pieces("r", RC, lo, hi), "pb": ["ef"] + pieces("vv", VC, lo, hi), "pc": ["ef", "ss%d" % k]}[a])
            return P.matmul(bank(k), T.nf[:] if a == "pa" else T.ef[:], {"pa": T.rr, "pb": T.vw, "pc": T.ss}[a][:, lo:hi], a == "pa", a == "pc")
        if a == "u":
            lo, hi = Y1[k], Y1[k + 1]
            after("ss%d" % k, *pieces("d", banks, lo, hi))
            return V.tensor_tensor(T.uu[:, lo:hi], gp(lo, hi), T.ss[:, lo:hi], Op.add)
        if a == "n":
            lo, hi = Y1[k], Y1[k + 1]
            after(("pc%d" if k in on_pe else "u%d") % k, "dd")
            return flip(q, T.uu[:, lo:hi], bank(k) if k in on_pe else T.uu[:, lo:hi], D)
        if a == "v":
            after("oi", *pieces("vv", VC))
            return gather(q, slot(T.sb3, k), T.vw[:, 0:n].indirect(cols(T.oi, turn[k], 128)))
        if a == "q":
            after("a3", "dd", "on")
            return flip(q, T.a0[:, Y0[k]:Y0[k + 1]], T.vw[:].indirect(T.oi[:, Y0[k] // 16:Y0[k + 1] // 16]), D)
        if a == "b":
            lo, hi = Y0[k], Y0[k + 1]
            after("q%d" % k, "xm0")
            if hi < n:
                after("b%d" % (k + 1))
            return V.tensor_tensor_scan(T.y0[:, back(lo, hi)], T.z0[:, hi:lo:-1], T.a0[:, back(lo, hi)],
                                        T.y0[:, hi:hi + 1] if hi < n else BIG, Op.max, Op.min)
        raise ValueError(w)

    def remote(w):
        if w == "mx":
            wait("g", "red")
            ids = [DstId(rid=topo.addr(cores[q])[0], pnc=topo.addr(cores[q])[1]) for q in turn]
            at = [HALF - 1 + 4 * j for j in range(N)]
            g.remote_dma_fused([RemoteDMATransfer(dst_ids=ids, dma_engine_mask=topo.mask(core, cores[turn[0]]), remote_sem=T.sem.a4,
                                                  srcs=[T.rb[:, at[0]:at[0] + 1]], dsts=[T.rb[:, j:j + 1] for j in at[1:]])], local_sem=T.sem.sent)
            sent[0] += engines(r, turn[0])
            return
        moves = []
        for a, k, part in parts(w):
            q = turn[k]
            j = N - 2 - k
            ready, dst, src, name = {"X": ([holds("x", k)], slot(T.cw, r, n), slot(T.sb1, k), "a1"),
                                     "H": (pieces("p", C2), slot(T.r2, j), slot(T.w2, q, SP + n), "a2%d" % j),
                                     "V": (["v%d" % k], slot(T.vw, j, n), slot(T.sb3, k), "a3")}[a]
            wait("g", *ready)
            rid, pid, _ = topo.addr(cores[q])
            use = topo.engines(core, cores[q])[part]
            moves.append(RemoteDMATransfer(dst_ids=[DstId(rid=rid, pnc=pid)], dma_engine_mask=sum(1 << e for e in use), remote_sem=T.sem[name], src=src, dst=dst))
            sent[0] += len(use)
        if len(moves) > 1:
            g.remote_dma_fused(moves, local_sem=T.sem.sent)
        else:
            g.remote_dma(dst, src, T.sem[name], T.sem.sent, pid, rid, topo.mask(core, cores[q]))

    done("l_hd", A.dma_start(T.hd[:], T.heads[:]))
    for w in LOADS.split():
        if w[0] == "i":
            wait("s", "fz")
            x = S.dma_start(T[w][::16, SP:SP + 4096], T.cw[:, n + r * CAP:n + r * CAP + 256])
        elif w[:2] == "d2":
            hi, lo = L2[int(w[2])], L2[int(w[2]) + 1]
            x = S.dma_start(T.d2[:, lo:hi], T.dur[:, 2 * n + lo:2 * n + hi])
        elif w[0] == "s":
            t = int(w[1]) - 1
            lo, hi, at = (r + 1, N, 0) if w[2] == "a" else (0, r, N - 1 - r)
            if lo == hi:
                continue
            x = S.dma_start(cols(T.la, at, 256 + t * SL, at + hi - lo - 1), cols(T.ship, lo, t * N * LC, hi - 1))
        elif w == "p2":
            x = S.dma_start(T.la[:, 0:128], T.prev[:, 128:])
        elif w == "p1":
            x = S.dma_start(T.la[:, 128:256], T.prev[:, 0:128])
        else:
            lo, hi = {"d0": (0, n), "d1": (n, 2 * n), "da": (n, 2 * n + 16), "db": (n - 1, 2 * n - 1)}[w]
            x = S.dma_start(T[w][:], T.dur[:, lo:hi])
        done("l_" + w, x)
    for q, names in (("v", VEC), ("a", ACT), ("p", PEQ)):
        for w in names.split():
            done(w, call(q, w))
    for w in POOL.split():
        if w[0] in "XHV" or w == "mx":
            remote(w)
        else:
            done(w, call("g", w))
    for w in STORES.split():
        if w[0] == "i":
            wait("s", *{"it": order["iw"], "ik": early, "iu": order["iv"]}[w])
            x = S.dma_start(T[w][:], (T.iw if w == "it" else T.iv)[::16, SP:SP + 4096])
        else:
            wait("s", w)
            cut, src, base = (Y1, T.uu, n) if w[0] == "n" else (Y0, T.y0, 0)
            lo, hi = cut[int(w[1])], cut[int(w[1]) + 1]
            x = S.dma_start(T.y[:, base + lo:base + hi], src[:, lo:hi])
        done("l_" + w, x)
    g.wait_ge(T.sem.sent, sent[0])
    wait("s", *[e for e in list(sems) if e not in waited])
